import numpy as np, ml_dtypes
CORES = [10,34,74,98]
N = 4
import mx_ref
BF = ml_dtypes.bfloat16
def pick(q, e):
    c = np.concatenate([q[0].reshape(128, -1, 4), np.zeros((128, 1, 4), np.uint8)], axis=1); s = np.concatenate([q[1], np.ones((16, 1), np.uint8)], axis=1)
    return (np.ascontiguousarray(c[:, e].reshape(128, -1)), np.ascontiguousarray(s[:, e]))
def join(*qs):
    return (np.concatenate([q[0] for q in qs], axis=1), np.concatenate([q[1] for q in qs], axis=1))
def put(q, e, v):
    c, s = q[0].reshape(128, -1, 4).copy(), q[1].copy(); c[:, e] = v[0].reshape(128, -1, 4); s[:, e] = v[1]
    return (c.reshape(128, -1), s)
def pk(c, s):
    return (np.ascontiguousarray(c), mx_ref.live(s))
def emit(q):
    return q[0], q[1]
def decode(q):
    o = []
    for b in range(4):
        e = np.zeros((128, 128, 4), np.float32); e[np.arange(128), np.arange(128), b] = 1
        o.append(mx_ref.matmul(mx_ref.quantize(e.reshape(128, 512).astype(BF)), q))
    return np.stack(o, axis=2).reshape(128, -1)
def cut(t, i, w=512):
    return t[:, w * i:w * i + w]
def f(rng, *shape):
    return mx_ref.flush((rng.standard_normal(shape, dtype=np.float32) * np.exp2(rng.integers(-2, 3, shape[:-1] + (1,)))).astype(BF))
def wide(rng, *shape, cols=0):
    v = rng.standard_normal(shape, dtype=np.float32) * np.exp2(rng.integers(-12, 13, shape)).astype(np.float32)
    if cols: v *= np.repeat(np.exp2(rng.integers(-cols, cols + 1, shape[:-2] + (1, shape[-1] // 4))) * (rng.random(shape[:-2] + (1, shape[-1] // 4)) > 0.0625), 4, axis=-1).astype(np.float32)
    return mx_ref.flush(v.astype(BF))
P, K, R, O = 384, 64, 2, 1
def big(v):
    v = v.astype(np.float32)
    v[np.abs(v) < np.float32(2.0 ** -16)] = 0
    return v.astype(BF)
def plain(rng):
    u = np.array(f(rng, N, 128, 512))
    u[:, :, 4 * R:] = 0
    return {"c": big(f(rng, N, 128, 4 * P)), "u": u, "w": f(rng, N, 128, 512 * O)}
def bf(v, *shape):
    return np.ascontiguousarray(v).reshape(shape).astype(np.float32).astype(BF)
def signs(rng):
    return rng.choice([-1.0, 1.0], (128, 1, 4))
def heavy(rng, way):
    d, g = plain(rng), signs(rng)
    size = np.exp2(rng.integers(0, 3, (N, P)))
    size[np.arange(N), rng.integers(0, P, N)] = 1024
    d["c"] = bf((1 + rng.random((N, 128, P, 4))) * size[:, None, :, None] * g * 2.0 ** 18, N, 128, 4 * P)
    d["u"][:, :, :4 * R] = bf((1 + rng.random((N, 128, R, 4))) * g * np.asarray(way)[:, None] * 2.0 ** 28, N, 128, 4 * R)
    return d
def setup_inputs(rng):
    return plain(rng)
def setup_inputs_one(rng):
    return heavy(rng, np.ones(R))
def setup_inputs_chain(rng):
    return heavy(rng, np.where(np.arange(R) == 0, 1.0, -1.0))
def setup_inputs_apart(rng):
    d, g = plain(rng), signs(rng)
    v = np.zeros((N, 128, P, 4))
    for r in range(N):
        at = rng.permutation(P)
        a, b = at[:K], at[K:2 * K]
        v[r][np.arange(K), a] = 32 * (1 + rng.random((K, 4)))
        v[r][np.arange(K), b] = 32 * (1 + rng.random((K, 4)))
        v[r][64:96, a] = -(1 + 0.125 * rng.random((32, K, 4)))
        v[r][64:96, at[K:]] = 4096
        v[r][96:, at[K:]] = 1 + rng.random((32, P - K, 4))
    d["c"] = bf(v * g * 2.0 ** 18, N, 128, 4 * P)
    q = (1 + rng.random((N, 128, R, 4))) * g
    q[:, :64] = 0
    d["u"][:, :, :4 * R] = bf(q, N, 128, 4 * R)
    return d
def setup_inputs_ties(rng):
    d, g = plain(rng), signs(rng)
    v = np.abs(d["c"].astype(np.float32)).reshape(N, 128, P, 4)[:, :, :8] * g
    v[:, :, 0] = 0
    h = [rng.permutation(np.arange(P) % 8) for r in range(N)]
    for r in range(0, N, 2):
        i = int(np.flatnonzero(h[r] == 0)[0])
        h[r][i] = h[r][0]
        h[r][0] = 0
    d["c"] = bf(np.stack([v[r][:, h[r]] for r in range(N)]), N, 128, 4 * P)
    d["u"][:, :, :4] = bf(np.abs(d["u"][:, :, :4].astype(np.float32)).reshape(N, 128, 1, 4) * g, N, 128, 4)
    return d
def setup_inputs_spread(rng):
    d = plain(rng)
    d["u"][:, :, 4:8] = 0
    return {**d, "c": big(wide(rng, N, 128, 4 * P, cols=6))}
def check_inputs(d):
    b = []
    for k, low in (("c", 2.0 ** -16), ("u", 2.0 ** -30), ("w", 2.0 ** -30)):
        v = np.abs(d[k].astype(np.float32))
        if not (np.isfinite(v).all() and ((v == 0) | (v >= low) & (v <= 2.0 ** 30)).all()): b.append("a value of " + k)
    if (d["u"][:, :, 4 * R:].astype(np.float32) != 0).any(): b.append("u has numbers behind its first R columns")
    return b
def reference(c, u, w):
    tg = np.zeros((N, R, K), np.float32)
    cs = [mx_ref.quantize(np.ascontiguousarray(c[r])) for r in range(N)]
    qu = [mx_ref.quantize(np.ascontiguousarray(u[r])) for r in range(N)]
    half, zero = np.float32(0.5), np.float32(0)
    for t in range(R):
        left, sent = [], []
        for r in range(N):
            s = mx_ref.matmul(qu[r], cs[r])[t] + zero
            left.append(np.argsort(s, kind="stable")[:K])
            sent.append(pick(cs[r], left[r]))
        for r in range(N):
            a = sent[r ^ (1 << t)]
            z = mx_ref.matmul(pick(a, np.concatenate([np.arange(K), np.full(128 - K, -1)])), cs[r])[:K] + zero
            z[:, left[r]] = -np.inf
            to = np.argmax(z, axis=1)
            merge = np.sort(np.unique(to, return_index=True)[1])
            fill = np.setdiff1d(np.arange(K), merge)
            places = np.sort(left[r])[:len(fill)]
            v = decode(join(cs[r], a)).reshape(128, P + K, 4)
            v[:, to[merge]] = half * v[:, to[merge]] + half * v[:, P + merge]
            new = mx_ref.quantize(np.ascontiguousarray(v[:, :P]).reshape(128, -1).astype(BF))
            q = put(cs[r], to[merge], pick(new, to[merge]))
            cs[r] = put(q, places, pick(a, fill))
            tg[r, t, merge] = to[merge]
            tg[r, t, fill] = -1 - places
    oc, osc, y = np.zeros((N, 128, 4 * P), np.uint8), np.zeros((N, 16, P), np.uint8), np.zeros((N, 128, O * P), np.float32)
    for r in range(N):
        oc[r], osc[r] = emit(cs[r])
        for o in range(O):
            y[r, :, o * P:o * P + P] = mx_ref.matmul(mx_ref.quantize(np.ascontiguousarray(cut(w[r], o))), cs[r])
    return {"oc": oc, "osc": osc, "tg": tg, "y": y}

@@ -1,0 +1,553 @@
+from concourse.mybir import dt, AluOpType as A, AxisListType, ActivationFunctionType as F
+
+F8, U8, BF, F32, U16 = "float8_e4m3fn_x4", "uint8", "bfloat16", "float32", "uint16"
+C16 = 12582912.0
+C32 = 402653184.0
+SCRATCH = {"ps": ("psum", [128, 4096], F32)}
+for _t, _l in (
+        (BF, "ct 1536 u8 8 ut 1024 wt 512 modb 128 lli 128 one 512 eb 520 w16 512 trs 512 whl 1024 "
+             "tri 128 idn 128 ngt 512 m8 8 cm 72 kb 24 kr 64 mk 1152 scn 576 xl 512 x1 512 xk 512 cap 384 jk 401 "
+             "xt 512 e0 1 gt 72 gb 72 mt 512 nb 512 tl 64 fm 512 bf 512 xm 608 af 512"),
+        (F32, "uf 8 pj 128 p1 1 k24 24 jb 4 h4 4 l4 4 yy 1 p16 1 pr1 1 bc 1 hb 1 vl 1 sc 3 sd 3 "
+              "th 384 tt 128 lv 3 lvs 3 n0 1 kh 64 zr 404 ix 1 i32 1 y1 1 t16 1 tab 64 xx 64 pl 1 qa 1 qb 1 ix16 1 "
+              "tgs 2 ysb 384 yw 512 hn 4 l5 4 nkh 1 rc 1 fl 1 sa 1 sb 1 nd 1 s0 1 a32 1 s2 1 nm 4"),
+        (U16, "ofl 4 ofr 24 oft 4 ofs 24"),
+        (F8, "uq 256 wq 128 kq 1408 xlq 128 x1q 128 xkq 128 xtq 128 fmq 128 afq 128 bfq 128 xmq 152 c0 384 c1 384 "
+             "c2 384 win0 576 win1 576 rep0 384 rep1 384 snd0 64 snd1 64"),
+        (U8, "us 256 ws 128 ks 1408 xls 128 x1s 128 xks 128 xts 128 fms 128 afs 128 bfs 128 xms 152 cs0 384 cs1 384 "
+             "cs2 384 wins0 576 wins1 576 reps0 384 reps1 384 snds0 64 snds1 64")):
+    _w = _l.split()
+    for _n, _c in zip(_w[::2], _w[1::2]):
+        SCRATCH[_n] = ("sbuf", [128, int(_c)], _t)
+NDMA = 24
+SEMAPHORES = ["sv", "ss", "st", "sp", "loc", "arr0", "arr1"] + ["d%d" % i for i in range(NDMA)]
+ONES, W16, TRS, WH, WL, EB, NEG, NB = 0, 128, 256, 384, 512, 640, 1152, 1280
+
+
+def rank_program(g, core, T, topo):
+    rank = T.rank_of(core)
+    if rank is None:
+        return
+    queue = {"v": g.vector, "s": g.scalar, "t": g.tensor, "p": g, "y": g.sync}
+    own = {"v": "sv", "s": "ss", "t": "st", "p": "sp"}
+    count = {s: 0 for s in SEMAPHORES}
+    clock = {}
+    known = {q: {} for q in queue}
+    hist = {}
+    ndma = [0]
+    part = [False]
+
+    def merge(a, b):
+        for s, v in b.items():
+            if a.get(s, 0) < v:
+                a[s] = v
+
+    def dep(q, rd, wr):
+        need = {}
+        for lst, w in ((rd, False), (wr, True)):
+            for reg in lst:
+                name, lo, hi = reg[0], reg[1], reg[2]
+                st = reg[3] if len(reg) > 3 else 1
+                psum = name == "ps"
+                if psum:
+                    lo, hi, st = lo // 512 * 512, (hi + 511) // 512 * 512, 1
+                for (l2, h2, s2, q2, w2, sem, val) in hist.get(name, ()):
+                    if l2 >= hi or lo >= h2 or (st == s2 and st > 1 and (lo - l2) % st):
+                        continue
+                    if psum and q == q2 and (q == "t" or not (w or w2)):
+                        continue
+                    if w or w2 or (psum and q != q2):
+                        need[sem] = max(need.get(sem, 0), val)
+        for sem in sorted(need, key=lambda s: s == own.get(q)):
+            if known[q].get(sem, 0) < need[sem]:
+                queue[q].wait_ge(T.sem[sem], need[sem])
+                merge(known[q], clock[(sem, need[sem])])
+
+    def note(q, rd, wr, sem, val):
+        c = dict(known[q])
+        c[sem] = val
+        if (sem, val - 1) in clock:
+            merge(c, clock[(sem, val - 1)])
+        clock[(sem, val)] = c
+        for lst, w in ((rd, False), (wr, True)):
+            for reg in lst:
+                name, lo, hi = reg[0], reg[1], reg[2]
+                st = reg[3] if len(reg) > 3 else 1
+                if name == "ps":
+                    lo, hi, st = lo // 512 * 512, (hi + 511) // 512 * 512, 1
+                hist.setdefault(name, []).append((lo, hi, st, q, w, sem, val))
+
+    def view(reg):
+        name, lo, hi = reg[0], reg[1], reg[2]
+        if len(reg) > 4:
+            return T[name][reg[4]:reg[5], lo:hi:reg[3]]
+        return T[name][:, lo:hi:reg[3]] if len(reg) > 3 else T[name][:, lo:hi]
+
+    def run(q, call, rd, wr):
+        dep(q, rd, wr)
+        sem = own[q]
+        count[sem] += 1
+        call().then_inc(T.sem[sem], 1)
+        note(q, rd, wr, sem, count[sem])
+
+    def whole(name):
+        return (name, 0, SCRATCH[name][1][1])
+
+    def R(x):
+        return whole(x) if isinstance(x, str) else x
+
+    def isreg(x):
+        return isinstance(x, (str, tuple))
+
+    def rows(x, p0, p1):
+        x = R(x)
+        return (x[0], x[1], x[2], x[3] if len(x) > 3 else 1, p0, p1)
+
+    def top(x):
+        return rows(x, 0, 64)
+
+    def low(x):
+        return rows(x, 64, 128)
+
+    def memset(o, v):
+        o = R(o)
+        run("v", lambda: g.vector.memset(view(o), v), [], [o])
+
+    def ts(o, i, s1, op0, s2=None, op1=None):
+        o, i = R(o), R(i)
+        rd = [i] + [R(s) for s in (s1, s2) if isreg(s)]
+        a = view(R(s1)) if isreg(s1) else s1
+        b = view(R(s2)) if isreg(s2) else s2
+        if op1 is None:
+            run("v", lambda: g.vector.tensor_scalar(view(o), view(i), a, None, op0), rd, [o])
+        else:
+            run("v", lambda: g.vector.tensor_scalar(view(o), view(i), a, b, op0, op1), rd, [o])
+
+    def tt(o, a, b, op):
+        o, a, b = R(o), R(a), R(b)
+        run("v", lambda: g.vector.tensor_tensor(view(o), view(a), view(b), op), [a, b], [o])
+
+    def cp(o, i):
+        o, i = R(o), R(i)
+        run("v", lambda: g.vector.tensor_copy(view(o), view(i)), [i], [o])
+
+    def red(o, i, op):
+        o, i = R(o), R(i)
+        run("v", lambda: g.vector.tensor_reduce(view(o), view(i), AxisListType.X, op), [i], [o])
+
+    def least(o, i):
+        o, i = R(o), R(i)
+        run("v", lambda: g.vector.tensor_reduce(view(o), view(i), AxisListType.X, A.min, apply_absolute_value=True),
+            [i], [o])
+
+    def scan(o, a, b, init, op0, op1):
+        o, a, b = R(o), R(a), R(b)
+        run("v", lambda: g.vector.tensor_tensor_scan(view(o), view(a), view(b), init, op0, op1), [a, b], [o])
+
+    def act(o, i, func, bias=None, scale=None, acc=None):
+        o, i = R(o), R(i)
+        rd, wr, kw = [i], [o], {}
+        for k, x in (("bias", bias), ("scale", scale)):
+            if isreg(x):
+                rd.append(R(x))
+                kw[k] = view(R(x))
+            elif x is not None:
+                kw[k] = x
+        if acc is not None:
+            wr.append(R(acc))
+            kw["accum_out"] = view(R(acc))
+        run("s", lambda: g.scalar.activation(view(o), view(i), func, **kw), rd, wr)
+
+    def quant(qn, sn, lo, n, src, slo):
+        s = (src, slo, slo + 4 * n)
+        run("v", lambda: g.vector.quantize_mx(T[qn][:, lo:lo + n], T[sn][:, lo:lo + n], view(s)),
+            [s], [(qn, lo, lo + n), (sn, lo, lo + n)])
+
+    def mm(bank, n, l, r, start=True, stop=True):
+        o = ("ps", 512 * bank, 512 * bank + n)
+        rl = [(l[0], l[2], l[2] + 128), (l[1], l[2], l[2] + 128), (r[0], r[2], r[2] + n), (r[1], r[2], r[2] + n)]
+        run("t", lambda: g.tensor.matmul_mx(view(o), view(rl[0]), view(rl[1]), view(rl[2]), view(rl[3]), start, stop),
+            rl, [o])
+
+    def pick_codes(o, olo, n, win, width, off, off0):
+        k = (off, off0, off0 + n // 16)
+        run("v", lambda: g.vector.tensor_copy(T[o][:, olo:olo + n].bitcast(dt.uint32),
+                                              T[win][:, 0:width].bitcast(dt.uint32).indirect(view(k))),
+            [(win, 0, width), k], [(o, olo, olo + n)])
+
+    def pick_rows(o, olo, n, win, width, off, off0):
+        k = (off, off0, off0 + n // 16)
+        run("s", lambda: g.scalar.activation(T[o][:, olo:olo + n], T[win][:, 0:width].indirect(view(k)), F.Copy),
+            [(win, 0, width), k], [(o, olo, olo + n)])
+
+    def pick(o, os, olo, n, win, wins, width, off, off0):
+        pick_codes(o, olo, n, win, width, off, off0)
+        pick_rows(os, olo, n, wins, width, off, off0)
+
+    def iota(o, pattern, base, cm, p0=0, p1=128):
+        o = R(o)
+        st = o[3] if len(o) > 3 else 1
+        if part[0] or p1 - p0 < 128:
+            g.wait_ge(T.sem["sp"], count["sp"])
+            merge(known["p"], clock[("sp", count["sp"])])
+        part[0] = p1 - p0 < 128
+        run("p", lambda: g.iota(T[o[0]][p0:p1, o[1]:o[2]:st], pattern, base, cm, allow_small_or_imprecise_dtypes=True),
+            [], [o])
+
+    def dma(q, out, in_, rd, wr):
+        dep(q, rd, wr)
+        sem = "d%d" % ndma[0]
+        ndma[0] += 1
+        count[sem] = 16
+        queue[q].dma_start(out, in_).then_inc(T.sem[sem], 16)
+        note(q, rd, wr, sem, 16)
+
+    K = ("kq", "ks")
+
+    dma("y", T.u8[:], T.u[:, 0:8], [], [whole("u8")])
+    dma("s", T.ct[:, 0:512], T.c[:, 0:512], [], [("ct", 0, 512)])
+    dma("y", T.ct[:, 512:1024], T.c[:, 512:1024], [], [("ct", 512, 1024)])
+    dma("s", T.ct[:, 1024:1536], T.c[:, 1024:1536], [], [("ct", 1024, 1536)])
+
+    iota("jb", [[128, 4]], 0, 1)
+    iota("p1", [[0, 1]], 1, 1)
+    iota("pj", [[1, 128]], 0, -1)
+    iota("lli", [[16, 4], [0, 2], [1, 16]], 0, 0)
+    iota("modb", [[0, 8], [1, 16]], 1, 0)
+    iota("k24", [[1, 24]], 0, 0)
+    iota("x1", [[0, 512]], 0, 0)
+    iota(("x1", 1, 320, 4), [[16, 5], [0, 16]], 0, 0, 0, 1)
+    iota(("x1", 2, 320, 4), [[0, 5], [1, 16]], 0, 0, 0, 1)
+    iota(("x1", 385, 480, 4), [[0, 24]], 0, 1, 0, 16)
+    iota(("x1", 385, 448, 4), [[16, 16]], 0, 0, 32, 48)
+    iota(("x1", 449, 480, 4), [[0, 8]], 240, 0, 32, 48)
+    iota(("x1", 449, 480, 4), [[16, 8]], 16, 0, 64, 80)
+    iota("kr", [[1, 64]], 0, 0)
+    iota(("ngt", 0, 256), [[0, 256]], -1, 0)
+    iota("e0", [[0, 1]], 1, -1)
+    memset("one", 1.0)
+    ts("h4", "jb", C32, A.add, C32, A.subtract)
+    ts("yy", "p1", -8.5, A.add, 0.0625, A.mult)
+    memset(("ngt", 256, 512), 0.0)
+    ts("tri", "pj", 0.0, A.is_lt)
+    tt("l4", "jb", "h4", A.subtract)
+    ts("p16", "yy", C16, A.add, C16, A.subtract)
+    for h, x in ((0, "h4"), (1, "l4")):
+        for b in range(4):
+            act(("whl", 512 * h + b, 512 * h + 512, 4), ("one", 0, 128), F.Copy, scale=(x, b, b + 1))
+    act(("xl", 3, 512, 4), ("one", 0, 128), F.Copy, scale=0.0)
+    act("nb", "one", F.Copy, scale=0.0)
+    quant(*K, ONES, 128, "one", 0)
+    ts("pr1", "p16", -16.0, A.mult, "p1", A.add)
+    ts("idn", "pj", 0.0, A.is_equal)
+    ts(("trs", 0, 512, 4), "pj", 0.0, A.is_gt)
+    ts(("w16", 0, 512, 4), "modb", "pr1", A.is_equal)
+    for e in range(4):
+        ts(("ut", e, 512, 4), ("one", 0, 128), ("u8", e, e + 1), A.mult)
+    quant("uq", "us", 0, 128, "ut", 0)
+
+    def scores(t, b):
+        c, s, u = "c%d" % t, "cs%d" % t, ("uq", "us", 128 * t)
+        mm(b, 128, (c, s, 128 * b), u)
+        mm(3 + b, 128, u, (c, s, 128 * b))
+
+    def column(b):
+        act(("sc", b, b + 1), ("ps", 512 * b, 512 * b + 1), F.Copy)
+
+    def spacing(b):
+        act(("sd", b, b + 1), ("ps", 512 * b, 512 * b + 1), F.Abs, bias=2.0 ** -120, scale=0.6 * 2.0 ** -23)
+
+    def threshold(b):
+        act(("th", 128 * b, 128 * b + 128), "tri", F.Identity, bias=("sc", b, b + 1), scale=("sd", b, b + 1))
+
+    for b in range(3):
+        quant("c0", "cs0", 128 * b, 128, "ct", 512 * b)
+        scores(0, b)
+    quant(*K, WH, 256, "whl", 0)
+    ts("m8", ("k24", 0, 8), "p16", A.is_equal, -512.0, A.mult)
+    ts("hn", "h4", -416.0, A.add, 2.0, A.mult)
+    ts("l5", "l4", 2.0, A.mult)
+
+    def constants_ranks():
+        for i in range(3):
+            act(("w16", i + 1, 512, 4), ("w16", 0, 512, 4), F.Copy)
+        for i in range(2):
+            act(("trs", i + 1, 512, 4), ("trs", 0, 512, 4), F.Copy)
+        act(("trs", 3, 512, 4), ("one", 0, 128), F.Copy)
+        act(("eb", 0, 512), "one", F.Copy, scale=0.0)
+
+    def constants_gap():
+        ts("rc", "p1", -64.0, A.add)
+        ts("bc", "p1", 447.0, A.add)
+        quant(*K, TRS, 128, "trs", 0)
+
+    def constants_nb():
+        act(("eb", 512, 520), ("one", 0, 8), F.Copy, scale=0.0)
+        for b in range(3):
+            act(("nb", 65 * b, 65 * b + 64, 8), "m8", F.Copy, scale=("hn", b, b + 1))
+            act(("nb", 65 * b + 4, 65 * b + 64, 8), "m8", F.Copy, scale=("l5", b, b + 1))
+            act(("nb", 192 + 33 * b, 224 + 33 * b, 4), "m8", F.Copy)
+
+    def own_side(s):
+        ts(low(("xm", 96 + s, 608, 4)), low("modb"), low("rc"), A.is_equal)
+
+    def constants_sent():
+        iota("xk", [[0, 512]], 0, 0)
+        iota(("xm", 0, 96, 4), [[128, 3], [0, 8]], 0, 0, 64, 128)
+        iota(("xm", 1, 96, 4), [[0, 3], [16, 8]], 0, 0, 64, 128)
+        iota(("xm", 2, 96, 4), [[0, 24]], 0, 1, 64, 128)
+        iota(("xm", 3, 96, 4), [[0, 24]], 0, 0, 64, 128)
+        iota("fm", [[0, 512]], 0, 0)
+        iota(("mt", 256, 512), [[0, 256]], 0, 0)
+        act(("eb", 4, 516, 4), "idn", F.Copy, scale=0.5)
+        act("kh", "kr", F.Copy, bias=0.5)
+        act(("cap", 64, 384), ("one", 0, 320), F.Copy, scale=1e29)
+
+    def constants_travel():
+        act(("cm", 0, 64), ("idn", 0, 64), F.Copy)
+        act(("cm", 64, 68), ("one", 0, 4), F.Copy, scale=0.0)
+        act("uf", "u8", F.Copy)
+        for e in range(4):
+            act(("ut", 512 + e, 1024, 4), ("one", 0, 128), F.Copy, scale=("uf", 4 + e, 5 + e))
+        ts(("cm", 68, 72), ("k24", 0, 4), "p16", A.is_equal)
+        quant(*K, NEG, 128, "ngt", 0)
+        act("gb", "cm", F.Copy, scale=40.0, bias=-40.0)
+        act(("xt", 259, 260), "e0", F.Relu)
+        act(("xt", 2, 288, 4), ("one", 0, 72), F.Copy, scale=16.0)
+        act("vl", "hb", F.Identity, scale=-1.0, bias="bc")
+        act("kb", "k24", F.Copy, scale=16.0, bias=-16.0)
+        act("nkh", "p1", F.Copy, scale=-1.0, bias=0.5)
+
+    for t in range(2):
+        c, cs, win, wins = "c%d" % t, "cs%d" % t, "win%d" % t, "wins%d" % t
+        rep, reps, snd, snds = "rep%d" % t, "reps%d" % t, "snd%d" % t, "snds%d" % t
+        nc, ncs = "c%d" % (t + 1), "cs%d" % (t + 1)
+        dma("y", T[win][:, 0:384].bitcast(dt.uint8), T[c][:, 0:384].bitcast(dt.uint8), [whole(c)], [(win, 0, 384)])
+        dma("y", T[wins][:, 0:384], T[cs][:, 0:384], [whole(cs)], [(wins, 0, 384)])
+        dma("y", T[win][:, 448:512].bitcast(dt.uint8), T[c][:, 0:64].bitcast(dt.uint8), [(c, 0, 64)], [(win, 448, 512)])
+        dma("y", T[wins][:, 448:512], T[cs][:, 0:64], [(cs, 0, 64)], [(wins, 448, 512)])
+
+        def against(b, d):
+            o, i = ("mk", 384 * b + 128 * d, 384 * b + 128 * d + 128), ("ps", 512 * (3 + d), 512 * (3 + d) + 128)
+            if b == d:
+                tt(o, i, ("th", 128 * b, 128 * b + 128), A.is_lt)
+            else:
+                ts(o, i, ("sc", b, b + 1), A.is_le if d < b else A.is_lt)
+
+        def total(b):
+            scan(("scn", 192 * b, 192 * b + 192), ("mk", 384 * b, 384 * b + 192), ("mk", 384 * b + 192, 384 * b + 384),
+                 0.0, A.add, A.add)
+
+        def onehot(b):
+            ts(("xl", b, 512, 4), "lli", ("scn", 192 * b + 191, 192 * b + 192), A.is_equal)
+
+        column(0)
+        if t == 0:
+            column(1)
+            spacing(0)
+            spacing(1)
+        else:
+            spacing(0)
+            column(1)
+            spacing(1)
+        threshold(0)
+        column(2)
+        spacing(2)
+        threshold(1)
+        threshold(2)
+        if t == 0:
+            constants_ranks()
+        for b, d in ((0, 1), (1, 0), (0, 2), (1, 2), (0, 0), (2, 0), (2, 1), (1, 1), (2, 2)):
+            against(b, d)
+        for b in range(3):
+            total(b)
+        for b in range(3):
+            onehot(b)
+        ranks = ("scn", 191, 576, 192)
+        ts("lv", ranks, 64.0, A.is_lt)
+        quant("xlq", "xls", 0, 128, "xl", 0)
+        mm(6, 128, K + (WH,), ("xlq", "xls", 0), True, False)
+        mm(6, 128, K + (WL,), ("xlq", "xls", 0), False, True)
+        for b in range(3):
+            act(("x1", 384 + 32 * b, 416 + 32 * b, 4), "m8", F.Copy, scale=("lv", b, b + 1))
+        ts(("x1", 320, 332, 4), ranks, 64.0, A.is_lt)
+        act(("x1", 327, 328), ("lv", 0, 1), F.Copy)
+        act(("x1", 331, 332), ("lv", 0, 1), F.Identity, bias=("lv", 1, 2))
+        ts(("x1", 0, 256, 4), ("idn", 0, 64), ("lv", 0, 1), A.mult, 512.0, A.mult)
+        act("lvs", "lv", F.Copy, scale=1.0 / 1024)
+        if t == 0:
+            constants_gap()
+            constants_nb()
+        run("v", lambda: g.vector.transpose(T.tt[:], T.ps[:, 3072:3200]), [("ps", 3072, 3200)], [whole("tt")])
+        quant("x1q", "x1s", 0, 128, "x1", 0)
+        cp("ofl", ("tt", 0, 128, 32))
+        if t == 0:
+            ts("hb", "bc", C32, A.add, C32, A.subtract)
+            ts("tl", ("pj", 0, 64), 0.0, A.is_ge)
+        pick(snd, snds, 0, 64, c, cs, 384, "ofl", 0)
+        dst = T.cores[rank ^ (1 << t)]
+        rid, pid, _ = topo.addr(dst)
+        m = topo.mask(core, dst)
+        ne = len(topo.engines(core, dst))
+        arr = "arr%d" % t
+        for o, s in ((win, snd), (wins, snds)):
+            dep("p", [whole(s)], [])
+            w, i = T[o][:, 384:448], T[s][:, 0:64]
+            if o == win:
+                w, i = w.bitcast(dt.uint8), i.bitcast(dt.uint8)
+            g.remote_dma(w, i, T.sem[arr], T.sem["loc"], pid, rid, m)
+            count["loc"] += ne
+        count[arr] = 2 * ne
+        clock[(arr, 2 * ne)] = {arr: 2 * ne}
+        for o in (win, wins):
+            hist.setdefault(o, []).append((384, 448, 1, "-", True, arr, 2 * ne))
+        if t == 0:
+            quant(*K, W16, 128, "w16", 0)
+            memset("xt", 0.0)
+            constants_sent()
+        else:
+            quant("wq", "ws", 0, 128, "wt", 0)
+        mm(7, 128, K + (ONES,), ("x1q", "x1s", 0))
+        mm(0, 128, K + (W16,), ("x1q", "x1s", 0))
+        red("n0", ("ps", 3584, 3649), A.min)
+        if t == 0:
+            own_side(0)
+            own_side(1)
+        ts("ofr", ("ps", 96, 120), "n0", A.max)
+        if t == 0:
+            own_side(2)
+            own_side(3)
+        pick(rep, reps, 0, 384, c, cs, 384, "ofr", 0)
+        mm(6, 128, K + (TRS,), ("x1q", "x1s", 0))
+        ts(("cap", 0, 64), "kh", "n0", A.subtract, 1e27, A.mult)
+        if t == 0:
+            memset(("zr", 3, 4), -1e29)
+            memset(("zr", 388, 404), 1e29)
+            constants_travel()
+            dma("y", T.wt[:], T.w[:], [], [whole("wt")])
+        else:
+            mm(5, 384, ("wq", "ws", 0), (c, cs, 0))
+            act(("yw", 0, 384), ("ps", 2560, 2944), F.Copy)
+        mm(1, 384, (win, wins, 384), (rep, reps, 0))
+        for b in range(3):
+            ts(("xk", b, 256, 4), "kr", ("ps", 3152 + b, 3153 + b), A.is_equal, ("lvs", b, b + 1), A.mult)
+        quant("xkq", "xks", 0, 128, "xk", 0)
+        if t == 0:
+            quant(*K, NB, 128, "nb", 0)
+            quant("uq", "us", 128, 128, "ut", 512)
+        mm(7, 128, ("xkq", "xks", 0), K + (W16,))
+        mm(0, 128, ("xkq", "xks", 0), K + (NB,))
+        mm(6, 128, K + (WH,), ("xkq", "xks", 0), True, False)
+        mm(6, 128, K + (WL,), ("xkq", "xks", 0), False, True)
+
+        def arrived(b):
+            if t == 0:
+                quant(*K, EB + 128 * b, 128, "eb", 4 - b)
+            mm(2 + b, 128, K + (EB + 128 * b,), (win, wins, 384), True, False)
+
+        if t == 1:
+            for b in range(4):
+                arrived(b)
+
+        def left_side(e):
+            act(("af", e, 512, 4), ("ps", 3584, 3712), F.Copy, scale=1024.0)
+
+        scan(("zr", 4, 388), ("ps", 512, 896), "cap", -1e29, A.max, A.min)
+        left_side(0)
+        left_side(1)
+        act("jk", ("zr", 3, 404), F.Sign, bias=("zr", 387, 388), scale=-1.0, acc="ix")
+        if t == 0:
+            arrived(0)
+        runs = ("mk", 0, 12)
+        ts(runs, ("zr", 35, 388, 32), ("zr", 387, 388), A.is_lt)
+        if t == 0:
+            arrived(1)
+        red("i32", runs, A.add)
+        if t == 0:
+            arrived(2)
+        ts("gt", "gb", "i32", A.subtract, 32.0, A.mult)
+        ts(("xt", 0, 288, 4), "cm", "i32", A.mult, 32.0, A.mult)
+        tt("tab", ("ps", 3072, 3136), "kr", A.add)
+        if t == 0:
+            act("bf", "one", F.Copy, scale=0.0)
+        left_side(2)
+        left_side(3)
+        act("s0", "i32", F.Identity, scale=-32.0, bias="hb")
+        act("a32", "i32", F.Copy, scale=32.0)
+        act("s2", "ix", F.Identity, scale=-1.0, bias="a32")
+        act("ix16", "ix", F.Copy, bias=16.0)
+        ts(("xt", 1, 288, 4), "gt", "ix", A.add, -16.0, A.max)
+        ts("y1", "ix", 7.5, A.add)
+        quant("xtq", "xts", 0, 128, "xt", 0)
+        mm(6, 128, K + (TRS,), ("xtq", "xts", 0), True, False)
+        mm(6, 128, ("xtq", "xts", 0), K + (NEG,), False, True)
+        mm(1, 128, K + (W16,), ("xtq", "xts", 0))
+        ts("t16", "y1", 16.0 * C16, A.add, 16.0 * C16 + 16.0, A.subtract)
+        if t == 0:
+            arrived(3)
+        else:
+            quant("afq", "afs", 0, 128, "af", 0)
+        for e in range(4):
+            ts(top(("xm", 96 + e, 608, 4)), top("modb"), top("t16"), A.add, top("ix"), A.is_equal)
+        least("nd", ("ps", 3072, 3137))
+        ts("oft", ("ps", 580, 584), -1.0, A.add)
+        ts(("fm", 0, 256, 4), "tl", "nd", A.is_gt)
+        quant("fmq", "fms", 0, 128, "fm", 0)
+        for b in (6, 7):
+            mm(b, 128, K + (ONES,), ("fmq", "fms", 0))
+        for e, x in ((0, "s0"), (1, "vl"), (2, "s2"), (3, -15.0)):
+            act(("nm", e, e + 1), "nd", F.Copy, scale=x)
+        pick(rep, reps, 0, 64, c, cs, 384, "oft", 0)
+        for e in range(4):
+            ts(top(("xm", e, 96, 4)), top("kb"), top("t16"), A.is_equal, top(("nm", e, e + 1)), A.mult)
+        for b in range(4):
+            mm(2 + b, 128, K + (EB + 128 * b,), (rep, reps, 0), False, True)
+        act(("jk", 0, 32), ("ps", 3072, 3104), F.Sign, bias="nkh", acc="sa")
+        act(("jk", 32, 64), ("ps", 3104, 3136), F.Sign, bias="nkh", acc="sb")
+        if t == 0:
+            quant("afq", "afs", 0, 128, "af", 0)
+        ts("fl", ("ps", 3647, 3648), "p1", A.is_ge)
+        mm(7, 128, ("fmq", "fms", 0), K + (ONES,))
+        for b in range(4):
+            act(("mt", b, 256, 4), ("ps", 512 * (2 + b), 512 * (2 + b) + 64), F.Copy)
+        act("qa", "nd", F.Copy, scale="ix16", bias=-1.0)
+        act("qb", "nd", F.Copy, scale=1024.0, bias=-1024.0)
+        quant("xmq", "xms", 0, 152, "xm", 0)
+        mm(1, 128, ("xmq", "xms", 24), ("xmq", "xms", 0), True, False)
+        run("v", lambda: g.vector.tensor_scalar(T.bf[:, 0:96:2], T.ps[:, 0:48], T.fl[:], None, A.mult),
+            [("ps", 0, 48), whole("fl")], [("bf", 0, 96, 4), ("bf", 2, 96, 4)])
+        ts(("bf", 1, 96, 4), ("ps", 48, 72), "sa", A.mult, "fl", A.mult)
+        ts(("bf", 3, 96, 4), ("ps", 48, 72), "sb", A.mult, "fl", A.mult)
+        quant("bfq", "bfs", 0, 128, "bf", 0)
+        mm(1, 128, ("afq", "afs", 0), ("bfq", "bfs", 0), False, True)
+        ts("xx", "tab", ("ps", 3584, 3585), A.subtract, 1.0, A.add)
+        quant(win, wins, 448, 128, "mt", 0)
+        least("pl", "xx")
+        cp("ofs", ("ps", 512, 536))
+        ts(("tgs", t, t + 1), "pl", "qb", A.mult, "qa", A.add)
+        if t == 0:
+            dma("y", T.tg[0, :], T.tgs[0:64, 0:1], [("tgs", 0, 1)], [])
+            for b in range(3):
+                pick(nc, ncs, 128 * b, 128, win, wins, 512, "ofs", 8 * b)
+                scores(1, b)
+        else:
+            mm(2, 128, ("wq", "ws", 0), (win, wins, 384))
+            act(("yw", 384, 512), ("ps", 1024, 1152), F.Copy)
+            pick_rows(ncs, 0, 192, wins, 512, "ofs", 0)
+            pick_rows("ysb", 192, 192, "yw", 512, "ofs", 12)
+            pick_rows(ncs, 192, 192, wins, 512, "ofs", 12)
+            for b in range(2):
+                pick_codes(nc, 192 * b, 192, win, 512, "ofs", 12 * b)
+                dma("y", T.oc[:, 768 * b:768 * b + 768], T[nc][:, 192 * b:192 * b + 192].bitcast(dt.uint8),
+                    [(nc, 192 * b, 192 * b + 192)], [])
+                if b == 0:
+                    dma("y", T.tg[1, :], T.tgs[0:64, 1:2], [("tgs", 1, 2)], [])
+                    dma("y", T.y[:, 192:384], T.ysb[:, 192:384], [("ysb", 192, 384)], [])
+            run("v", lambda: g.vector.tensor_copy(T.ysb[:, 0:192], T.yw[:].indirect(T.ofs[:, 0:12])),
+                [whole("yw"), ("ofs", 0, 12)], [("ysb", 0, 192)])
+            for k in range(4):
+                dma("s", T.osc[4 * k:4 * k + 4, :], T[ncs][32 * k:32 * k + 4, 0:384], [whole(ncs)], [])
+            dma("y", T.y[:, 0:192], T.ysb[:, 0:192], [("ysb", 0, 192)], [])
+    for s in SEMAPHORES:
+        if count[s]:
+            g.wait_ge(T.sem[s], count[s])

@@ -5,23 +5,32 @@ C16 = 12582912.0
 C32 = 402653184.0
 SCRATCH = {"ps": ("psum", [128, 4096], F32)}
 for _t, _l in (
-        (BF, "ct 1536 u8 8 ut 1024 wt 512 modb 128 lli 128 one 512 eb 520 w16 512 trs 512 whl 1024 "
-             "tri 128 idn 128 ngt 512 m8 8 cm 72 kb 24 kr 64 mk 1152 scn 576 xl 512 x1 512 xk 512 cap 384 jk 401 "
-             "xt 512 e0 1 gt 72 gb 72 mt 512 nb 512 tl 64 fm 512 bf 512 xm 608 af 512"),
-        (F32, "uf 8 pj 128 p1 1 k24 24 jb 4 h4 4 l4 4 yy 1 p16 1 pr1 1 bc 1 hb 1 vl 1 sc 3 sd 3 "
-              "th 384 tt 128 lv 3 lvs 3 n0 1 kh 64 zr 404 ix 1 i32 1 y1 1 t16 1 tab 64 xx 64 pl 1 qa 1 qb 1 ix16 1 "
-              "tgs 2 ysb 384 yw 512 hn 4 l5 4 nkh 1 rc 1 fl 1 sa 1 sb 1 nd 1 s0 1 a32 1 s2 1 nm 4"),
-        (U16, "ofl 4 ofr 24 oft 4 ofs 24"),
-        (F8, "uq 256 wq 128 kq 1408 xlq 128 x1q 128 xkq 128 xtq 128 fmq 128 afq 128 bfq 128 xmq 152 c0 384 c1 384 "
-             "c2 384 win0 576 win1 576 rep0 384 rep1 384 snd0 64 snd1 64"),
-        (U8, "us 256 ws 128 ks 1408 xls 128 x1s 128 xks 128 xts 128 fms 128 afs 128 bfs 128 xms 152 cs0 384 cs1 384 "
-             "cs2 384 wins0 576 wins1 576 reps0 384 reps1 384 snds0 64 snds1 64")):
+        (BF, "ct 1536 u8 8 ut 1024 wt 512 modb 128 lli 128 xo 536 eb 520 mw 768 ft 1536 "
+             "tri 128 idn 64 m8 8 cm 4 kb 24 kr 64 mk 1152 scn 576 xl 512 x1 512 cap 384 jk 392 "
+             "gb 4 nb 512 tl 64 xm 608 ne 64 whl 1024 h16 80 mod9 128"),
+        (F32, "pj 128 p1 1 k24 24 jb 4 h4 4 l4 4 yy 1 p16 1 pr1 1 bc 1 sc 3 sd 3 "
+              "th 384 tt 128 lv 3 lw 3 n0 1 kh 64 zr 392 ix 1 i32 1 y2 1 t16 1 xx 64 tab 64 pl 1 qa 1 qb 1 "
+              "tgs 2 ysb 384 yw 576 hn 4 l5 4 nd 1 v0 1 v1 1 vh 1 vw 1 ixn 1 msk 32 tin 64 tou 64 "
+              "ska 1 skb 1 kc 4 nk 4 ac 4 fl 4 ff 4 al 4 m240 1 gt 4"),
+        (U16, "ofl 4 ofr 24 oft 4 ofa 4 ofs 24"),
+        (F8, "uq 256 wq 128 kq 1408 xlq 128 x1q 128 xkq 256 xtq 128 fmq 128 xmq 152 c0 384 c1 384 "
+             "c2 384 wina0 448 wina1 448 winb0 576 winb1 576 rep0 384 rep1 384 snd0 64 snd1 64"),
+        (U8, "us 256 ws 128 ks 1408 xls 128 x1s 128 xks 256 xts 128 fms 128 xms 152 cs0 384 cs1 384 "
+             "cs2 384 winas0 448 winas1 448 winbs0 576 winbs1 576 reps0 384 reps1 384 snds0 64 snds1 64")):
     _w = _l.split()
     for _n, _c in zip(_w[::2], _w[1::2]):
         SCRATCH[_n] = ("sbuf", [128, int(_c)], _t)
 NDMA = 24
 SEMAPHORES = ["sv", "ss", "st", "sp", "loc", "arr0", "arr1"] + ["d%d" % i for i in range(NDMA)]
-ONES, W16, TRS, WH, WL, EB, NEG, NB = 0, 128, 256, 384, 512, 640, 1152, 1280
+ONES, W16, TRS, WH, WL, EB, NB = 0, 128, 256, 384, 512, 640, 1280
+PARTS = {"xt": ("xo", 0, 16), "one": ("xo", 16, 536), "fm": ("ft", 0, 256), "trs": ("ft", 256, 768),
+         "xk": ("ft", 512, 1536), "mt": ("mw", 0, 256), "w16": ("mw", 256, 768)}
+SMALL = [_n for _n, _v in SCRATCH.items() if _v[2] == F32 and _v[1][1] <= 4 and _n != "tgs"]
+SCRATCH["sm"] = ("sbuf", [128, 4 * len(SMALL)], F32)
+for _i, _n in enumerate(SMALL):
+    PARTS[_n] = ("sm", 4 * _i, 4 * _i + SCRATCH.pop(_n)[1][1])
+QUEUES = "ssvsssssvsssssssssssssssssvssssssssssssssssssssssssssssssssssssssssssssssssssvvsssssvssssvsssvssssssssssvssvsvssssssvssvsvvsssssvvssvssvvvsvssvv"
+ORDER = """12 5 0 23 49 1 4 2 3 6 35 47 34 13 15 39 71 155 38 37 9 169 53 36 41 251 58 55 56 40 42 48 44 57 46 60 8 16 7 59 250 63 252 28 45 43 70 168 139 27 61 64 65 62 77 66 69 79 78 81 91 92 95 80 173 67 68 82 94 93 97 83 74 76 73 84 98 72 85 21 96 99 101 100 102 89 30 104 172 52 18 128 20 103 88 122 14 19 154 105 132 108 112 115 54 109 111 106 110 114 26 129 17 11 10 24 127 120 124 116 131 113 75 133 145 117 90 86 22 87 135 200 171 25 107 134 138 123 51 119 130 140 149 137 150 142 31 143 162 160 141 146 157 161 136 158 147 29 32 118 33 121 199 153 125 126 201 148 159 151 156 50 163 182 174 197 185 167 186 170 144 180 176 179 206 187 152 189 175 202 192 183 164 165 190 205 207 203 191 208 177 209 178 211 166 198 212 193 210 181 204 213 194 195 217 228 184 196 214 218 219 188 230 215 216 229 236 237 231 253 222 224 220 233 238 240 226 239 232 234 254 241 243 225 221 223 235 227 242 249 248 247 260 246 264 255 259 263 261 267 265 266 256 268 275 271 274 318 270 269 284 262 277 276 278 280 286 281 287 285 282 279 290 289 283 245 291 244 288 292 294 327 293 295 297 296 298 306 301 272 309 273 302 299 307 305 304 308 310 303 311 312 319 313 257 314 328 300 325 320 321 334 322 335 316 315 317 333 324 330 323 332 331 329 326 336 340 341 345 348 337 338 346 342 350 367 352 353 363 339 343 347 365 351 355 356 370 344 371 357 372 373 374 359 366 364 376 375 361 349 358 377 360 368 378 382 393 369 379 380 362 383 381 384 395 394 391 389 354 402 401 398 399 397 396 385 403 405 387 400 404 386 392 390 258 408 409 410 388 406 415 413 407 419 414 416 420 421 411 417 423 418 427 412 430 425 428 422 429 435 426 424 431 433 432 434"""
 
 
 def rank_program(g, core, T, topo):
@@ -35,24 +44,27 @@ def rank_program(g, core, T, topo):
     known = {q: {} for q in queue}
     hist = {}
     ndma = [0]
-    part = [False]
+    turns = [0]
+    calls = []
 
     def merge(a, b):
         for s, v in b.items():
             if a.get(s, 0) < v:
                 a[s] = v
 
+    def span(reg):
+        if reg[0] == "ps":
+            return reg[1] // 512 * 512, (reg[2] + 511) // 512 * 512, 1, 0, 128
+        return (reg[1], reg[2], reg[3] if len(reg) > 3 else 1) + (tuple(reg[4:]) or (0, 128))
+
     def dep(q, rd, wr):
         need = {}
         for lst, w in ((rd, False), (wr, True)):
             for reg in lst:
-                name, lo, hi = reg[0], reg[1], reg[2]
-                st = reg[3] if len(reg) > 3 else 1
-                psum = name == "ps"
-                if psum:
-                    lo, hi, st = lo // 512 * 512, (hi + 511) // 512 * 512, 1
-                for (l2, h2, s2, q2, w2, sem, val) in hist.get(name, ()):
-                    if l2 >= hi or lo >= h2 or (st == s2 and st > 1 and (lo - l2) % st):
+                psum = reg[0] == "ps"
+                lo, hi, st, p0, p1 = span(reg)
+                for (l2, h2, s2, p2, p3, q2, w2, sem, val) in hist.get(reg[0], ()):
+                    if l2 >= hi or lo >= h2 or p2 >= p1 or p0 >= p3 or (st == s2 and st > 1 and (lo - l2) % st):
                         continue
                     if psum and q == q2 and (q == "t" or not (w or w2)):
                         continue
@@ -71,11 +83,7 @@ def rank_program(g, core, T, topo):
         clock[(sem, val)] = c
         for lst, w in ((rd, False), (wr, True)):
             for reg in lst:
-                name, lo, hi = reg[0], reg[1], reg[2]
-                st = reg[3] if len(reg) > 3 else 1
-                if name == "ps":
-                    lo, hi, st = lo // 512 * 512, (hi + 511) // 512 * 512, 1
-                hist.setdefault(name, []).append((lo, hi, st, q, w, sem, val))
+                hist.setdefault(reg[0], []).append(span(reg) + (q, w, sem, val))
 
     def view(reg):
         name, lo, hi = reg[0], reg[1], reg[2]
@@ -84,17 +92,24 @@ def rank_program(g, core, T, topo):
         return T[name][:, lo:hi:reg[3]] if len(reg) > 3 else T[name][:, lo:hi]
 
     def run(q, call, rd, wr):
-        dep(q, rd, wr)
-        sem = own[q]
-        count[sem] += 1
-        call().then_inc(T.sem[sem], 1)
-        note(q, rd, wr, sem, count[sem])
+        def issue():
+            dep(q, rd, wr)
+            sem = own[q]
+            count[sem] += 1
+            call().then_inc(T.sem[sem], 1)
+            note(q, rd, wr, sem, count[sem])
+        calls.append((q, issue, rd, wr))
 
     def whole(name):
-        return (name, 0, SCRATCH[name][1][1])
+        return PARTS[name] if name in PARTS else (name, 0, SCRATCH[name][1][1])
 
     def R(x):
-        return whole(x) if isinstance(x, str) else x
+        if isinstance(x, str):
+            return whole(x)
+        if x[0] in PARTS:
+            name, lo, _ = PARTS[x[0]]
+            return (name, lo + x[1], lo + x[2]) + tuple(x[3:])
+        return x
 
     def isreg(x):
         return isinstance(x, (str, tuple))
@@ -109,19 +124,31 @@ def rank_program(g, core, T, topo):
     def low(x):
         return rows(x, 64, 128)
 
+    def bank(b, lo, hi):
+        return ("ps", 512 * b + lo, 512 * b + hi)
+
+    def either():
+        turns[0] += 1
+        return QUEUES[turns[0] - 1]
+
     def memset(o, v):
         o = R(o)
-        run("v", lambda: g.vector.memset(view(o), v), [], [o])
+        if o != R("one") and either() == "s":
+            i = R(("one", 0, len(range(*span(o)[:3])), 1) + span(o)[3:])
+            run("s", lambda: g.scalar.activation(view(o), view(i), F.Copy, scale=0.0, bias=v), [i], [o])
+        else:
+            run("v", lambda: g.vector.memset(view(o), v), [], [o])
 
-    def ts(o, i, s1, op0, s2=None, op1=None):
+    def ts(o, i, s1, op0, s2=None, op1=None, wr=None):
         o, i = R(o), R(i)
+        wr = wr or [o]
         rd = [i] + [R(s) for s in (s1, s2) if isreg(s)]
         a = view(R(s1)) if isreg(s1) else s1
         b = view(R(s2)) if isreg(s2) else s2
         if op1 is None:
-            run("v", lambda: g.vector.tensor_scalar(view(o), view(i), a, None, op0), rd, [o])
+            run("v", lambda: g.vector.tensor_scalar(view(o), view(i), a, None, op0), rd, wr)
         else:
-            run("v", lambda: g.vector.tensor_scalar(view(o), view(i), a, b, op0, op1), rd, [o])
+            run("v", lambda: g.vector.tensor_scalar(view(o), view(i), a, b, op0, op1), rd, wr)
 
     def tt(o, a, b, op):
         o, a, b = R(o), R(a), R(b)
@@ -144,9 +171,17 @@ def rank_program(g, core, T, topo):
         o, a, b = R(o), R(a), R(b)
         run("v", lambda: g.vector.tensor_tensor_scan(view(o), view(a), view(b), init, op0, op1), [a, b], [o])
 
-    def act(o, i, func, bias=None, scale=None, acc=None):
+    def turn(o, i):
         o, i = R(o), R(i)
-        rd, wr, kw = [i], [o], {}
+        run("v", lambda: g.vector.transpose(view(o), view(i)), [i], [o])
+
+    def act(o, i, func, bias=None, scale=None, acc=None, wr=None):
+        o, i = R(o), R(i)
+        if func in (F.Copy, F.Identity) and either() == "v":
+            if bias is None:
+                return ts(o, i, 1.0 if scale is None else scale, A.mult, wr=wr)
+            return ts(o, i, 1.0 if scale is None else scale, A.mult, bias, A.add, wr=wr)
+        rd, wr, kw = [i], wr or [o], {}
         for k, x in (("bias", bias), ("scale", scale)):
             if isreg(x):
                 rd.append(R(x))
@@ -159,50 +194,76 @@ def rank_program(g, core, T, topo):
         run("s", lambda: g.scalar.activation(view(o), view(i), func, **kw), rd, wr)
 
     def quant(qn, sn, lo, n, src, slo):
-        s = (src, slo, slo + 4 * n)
+        s = R((src, slo, slo + 4 * n))
         run("v", lambda: g.vector.quantize_mx(T[qn][:, lo:lo + n], T[sn][:, lo:lo + n], view(s)),
             [s], [(qn, lo, lo + n), (sn, lo, lo + n)])
 
-    def mm(bank, n, l, r, start=True, stop=True):
-        o = ("ps", 512 * bank, 512 * bank + n)
+    def mm(b, n, l, r, start=True, stop=True):
+        o = bank(b, 0, n)
         rl = [(l[0], l[2], l[2] + 128), (l[1], l[2], l[2] + 128), (r[0], r[2], r[2] + n), (r[1], r[2], r[2] + n)]
         run("t", lambda: g.tensor.matmul_mx(view(o), view(rl[0]), view(rl[1]), view(rl[2]), view(rl[3]), start, stop),
             rl, [o])
 
-    def pick_codes(o, olo, n, win, width, off, off0):
+    def pick_codes(o, olo, n, win, wide, off, off0):
         k = (off, off0, off0 + n // 16)
         run("v", lambda: g.vector.tensor_copy(T[o][:, olo:olo + n].bitcast(dt.uint32),
-                                              T[win][:, 0:width].bitcast(dt.uint32).indirect(view(k))),
-            [(win, 0, width), k], [(o, olo, olo + n)])
+                                              T[win][:, 0:wide].bitcast(dt.uint32).indirect(view(k))),
+            [(win, 0, wide), k], [(o, olo, olo + n)])
 
-    def pick_rows(o, olo, n, win, width, off, off0):
+    def pick_rows(o, olo, n, win, wide, off, off0, lo=0):
+        q = either()
         k = (off, off0, off0 + n // 16)
-        run("s", lambda: g.scalar.activation(T[o][:, olo:olo + n], T[win][:, 0:width].indirect(view(k)), F.Copy),
-            [(win, 0, width), k], [(o, olo, olo + n)])
+        rd, wr = [(win, lo, lo + wide), k], [(o, olo, olo + n)]
+        if q == "s":
+            run(q, lambda: g.scalar.activation(view(wr[0]), view(rd[0]).indirect(view(k)), F.Copy), rd, wr)
+        else:
+            run(q, lambda: g.vector.tensor_copy(view(wr[0]), view(rd[0]).indirect(view(k))), rd, wr)
 
-    def pick(o, os, olo, n, win, wins, width, off, off0):
-        pick_codes(o, olo, n, win, width, off, off0)
-        pick_rows(os, olo, n, wins, width, off, off0)
+    def pick(o, os, olo, n, win, wins, wide, off, off0):
+        pick_codes(o, olo, n, win, wide, off, off0)
+        pick_rows(os, olo, n, wins, wide, off, off0)
 
-    def iota(o, pattern, base, cm, p0=0, p1=128):
+    def iota(o, pattern, base, cm):
         o = R(o)
-        st = o[3] if len(o) > 3 else 1
-        if part[0] or p1 - p0 < 128:
-            g.wait_ge(T.sem["sp"], count["sp"])
-            merge(known["p"], clock[("sp", count["sp"])])
-        part[0] = p1 - p0 < 128
-        run("p", lambda: g.iota(T[o[0]][p0:p1, o[1]:o[2]:st], pattern, base, cm, allow_small_or_imprecise_dtypes=True),
-            [], [o])
+        run("p", lambda: g.iota(view(o), pattern, base, cm, allow_small_or_imprecise_dtypes=True), [], [o])
+
+    def select(o, pattern, op, base, cm):
+        o = R(o)
+        i = R(("one", 0, len(range(*span(o)[:3]))))
+        run("p", lambda: g.affine_select(view(o), view(i), pattern, op, 0.0, base, cm), [i], [o])
 
     def dma(q, out, in_, rd, wr):
-        dep(q, rd, wr)
-        sem = "d%d" % ndma[0]
-        ndma[0] += 1
-        count[sem] = 16
-        queue[q].dma_start(out, in_).then_inc(T.sem[sem], 16)
-        note(q, rd, wr, sem, 16)
+        q = q or ("s" if either() == "s" else "y")
+
+        def issue():
+            dep(q, rd, wr)
+            sem = "d%d" % ndma[0]
+            ndma[0] += 1
+            count[sem] = 16
+            queue[q].dma_start(out, in_).then_inc(T.sem[sem], 16)
+            note(q, rd, wr, sem, 16)
+        calls.append((q, issue, rd, wr))
+
+    def send(t, o, s, codes):
+        dst = T.cores[rank ^ (1 << t)]
+        rid, pid, _ = topo.addr(dst)
+        ne = len(topo.engines(core, dst))
+        arr = "arr%d" % t
+
+        def issue():
+            dep("p", [whole(s)], [])
+            w, i = T[o][:, 0:64], T[s][:, 0:64]
+            if codes:
+                w, i = w.bitcast(dt.uint8), i.bitcast(dt.uint8)
+            g.remote_dma(w, i, T.sem[arr], T.sem["loc"], pid, rid, topo.mask(core, dst))
+            count["loc"] += ne
+            count[arr] = 2 * ne
+            clock[(arr, 2 * ne)] = {arr: 2 * ne}
+            hist.setdefault(o, []).append((0, 64, 1, 0, 128, "-", True, arr, 2 * ne))
+        calls.append(("p", issue, [whole(s)], [(o, 0, 64)]))
 
     K = ("kq", "ks")
+    one128 = ("one", 0, 128)
 
     dma("y", T.u8[:], T.u[:, 0:8], [], [whole("u8")])
     dma("s", T.ct[:, 0:512], T.c[:, 0:512], [], [("ct", 0, 512)])
@@ -215,35 +276,53 @@ def rank_program(g, core, T, topo):
     iota("lli", [[16, 4], [0, 2], [1, 16]], 0, 0)
     iota("modb", [[0, 8], [1, 16]], 1, 0)
     iota("k24", [[1, 24]], 0, 0)
-    iota("x1", [[0, 512]], 0, 0)
-    iota(("x1", 1, 320, 4), [[16, 5], [0, 16]], 0, 0, 0, 1)
-    iota(("x1", 2, 320, 4), [[0, 5], [1, 16]], 0, 0, 0, 1)
-    iota(("x1", 385, 480, 4), [[0, 24]], 0, 1, 0, 16)
-    iota(("x1", 385, 448, 4), [[16, 16]], 0, 0, 32, 48)
-    iota(("x1", 449, 480, 4), [[0, 8]], 240, 0, 32, 48)
-    iota(("x1", 449, 480, 4), [[16, 8]], 16, 0, 64, 80)
     iota("kr", [[1, 64]], 0, 0)
-    iota(("ngt", 0, 256), [[0, 256]], -1, 0)
-    iota("e0", [[0, 1]], 1, -1)
+    iota("h16", [[16, 5], [0, 16]], 0, 0)
     memset("one", 1.0)
+    memset(("xk", 259, 1024, 4), 0.0)
+    memset("fm", 0.0)
+    memset("x1", 0.0)
+    select("eb", [[1, 520]], A.is_equal, -4, -4)
+    select(("trs", 0, 512, 4), [[1, 128]], A.is_gt, 0, -1)
+    for e in (1, 2, 3):
+        memset(("trs", e, 512, 4), 1.0)
+    memset(top(("xm", 0, 96)), 0.0)
+    memset(rows(("tin", 32, 64), 0, 32), 1000.0)
+
+    def places(x, lo, n, row):
+        act(rows((x, lo, lo + 4 * n - 3, 4), 0, 1), rows(("h16", 0, n), 0, 1), F.Copy)
+        act(rows((x, lo, lo + 4 * n - 3, 4), row, row + 1), rows(("modb", 0, n), row, row + 1), F.Copy, bias=-1.0)
+
+    def offsets(x, lo):
+        ts(rows((x, lo, lo + 95, 4), 0, 16), rows("k24", 0, 16), 16.0, A.mult, 240.0, A.min)
+        act(rows((x, lo + 1, lo + 95, 4), 0, 16), rows("k24", 0, 16), F.Relu, scale=16.0, bias=rows("m240", 0, 16))
+        act(rows((x, lo, lo + 95, 4), 32, 48), rows(("one", 0, 24), 32, 48), F.Copy, scale=rows("p1", 32, 48), bias=-33.0)
+
+    memset("m240", -240.0)
+    places("x1", 1, 80, 32)
+    offsets("x1", 385)
+    places("xk", 259, 64, 32)
+    offsets("xm", 2)
     ts("h4", "jb", C32, A.add, C32, A.subtract)
-    ts("yy", "p1", -8.5, A.add, 0.0625, A.mult)
-    memset(("ngt", 256, 512), 0.0)
+    act("yy", "p1", F.Copy, scale=0.0625, bias=-8.5 / 16)
     ts("tri", "pj", 0.0, A.is_lt)
     tt("l4", "jb", "h4", A.subtract)
     ts("p16", "yy", C16, A.add, C16, A.subtract)
     for h, x in ((0, "h4"), (1, "l4")):
-        for b in range(4):
-            act(("whl", 512 * h + b, 512 * h + 512, 4), ("one", 0, 128), F.Copy, scale=(x, b, b + 1))
-    act(("xl", 3, 512, 4), ("one", 0, 128), F.Copy, scale=0.0)
-    act("nb", "one", F.Copy, scale=0.0)
+        for b in range(3):
+            act(("whl", 512 * h + b, 512 * h + 512, 4), one128, F.Copy, scale=(x, b, b + 1))
+    memset(("whl", 3, 512, 4), 1024.0)
+    memset(("whl", 515, 1024, 4), 0.0)
+    memset(("w16", 3, 512, 4), 0.0)
+    memset(("xl", 3, 512, 4), 0.0)
+    memset("nb", 0.0)
+    memset(("nb", 320, 321), 1024.0)
     quant(*K, ONES, 128, "one", 0)
-    ts("pr1", "p16", -16.0, A.mult, "p1", A.add)
-    ts("idn", "pj", 0.0, A.is_equal)
-    ts(("trs", 0, 512, 4), "pj", 0.0, A.is_gt)
+    act("pr1", "p16", F.Identity, scale=-16.0, bias="p1")
+    ts("idn", ("pj", 0, 64), 0.0, A.is_equal, 64.0, A.mult)
     ts(("w16", 0, 512, 4), "modb", "pr1", A.is_equal)
     for e in range(4):
-        ts(("ut", e, 512, 4), ("one", 0, 128), ("u8", e, e + 1), A.mult)
+        ts(("ut", e, 512, 4), one128, ("u8", e, e + 1), A.mult)
     quant("uq", "us", 0, 128, "ut", 0)
 
     def scores(t, b):
@@ -252,10 +331,10 @@ def rank_program(g, core, T, topo):
         mm(3 + b, 128, u, (c, s, 128 * b))
 
     def column(b):
-        act(("sc", b, b + 1), ("ps", 512 * b, 512 * b + 1), F.Copy)
+        act(("sc", b, b + 1), bank(b, 0, 1), F.Copy)
 
     def spacing(b):
-        act(("sd", b, b + 1), ("ps", 512 * b, 512 * b + 1), F.Abs, bias=2.0 ** -120, scale=0.6 * 2.0 ** -23)
+        act(("sd", b, b + 1), bank(b, 0, 1), F.Abs, bias=2.0 ** -120, scale=0.6 * 2.0 ** -23)
 
     def threshold(b):
         act(("th", 128 * b, 128 * b + 128), "tri", F.Identity, bias=("sc", b, b + 1), scale=("sd", b, b + 1))
@@ -264,71 +343,45 @@ def rank_program(g, core, T, topo):
         quant("c0", "cs0", 128 * b, 128, "ct", 512 * b)
         scores(0, b)
     quant(*K, WH, 256, "whl", 0)
-    ts("m8", ("k24", 0, 8), "p16", A.is_equal, -512.0, A.mult)
-    ts("hn", "h4", -416.0, A.add, 2.0, A.mult)
-    ts("l5", "l4", 2.0, A.mult)
+    ts("m8", ("k24", 0, 8), "p16", A.is_equal, 64.0, A.mult)
+    act("hn", "h4", F.Copy, scale=-1.0 / 64, bias=6.5)
+    act("l5", "l4", F.Copy, scale=-1.0 / 64)
 
     def constants_ranks():
-        for i in range(3):
-            act(("w16", i + 1, 512, 4), ("w16", 0, 512, 4), F.Copy)
         for i in range(2):
-            act(("trs", i + 1, 512, 4), ("trs", 0, 512, 4), F.Copy)
-        act(("trs", 3, 512, 4), ("one", 0, 128), F.Copy)
-        act(("eb", 0, 512), "one", F.Copy, scale=0.0)
+            act(("w16", i + 1, 512, 4), ("w16", 0, 512, 4), F.Copy)
+        act("kb", "k24", F.Copy, scale=16.0, bias=16.0)
+        act("mod9", "modb", F.Copy, bias=-9.0)
+        act("kc", ("kb", 0, 4), F.Identity, bias="pr1")
 
     def constants_gap():
-        ts("rc", "p1", -64.0, A.add)
-        ts("bc", "p1", 447.0, A.add)
+        act("bc", "p1", F.Copy, bias=455.0)
         quant(*K, TRS, 128, "trs", 0)
 
     def constants_nb():
-        act(("eb", 512, 520), ("one", 0, 8), F.Copy, scale=0.0)
         for b in range(3):
             act(("nb", 65 * b, 65 * b + 64, 8), "m8", F.Copy, scale=("hn", b, b + 1))
             act(("nb", 65 * b + 4, 65 * b + 64, 8), "m8", F.Copy, scale=("l5", b, b + 1))
-            act(("nb", 192 + 33 * b, 224 + 33 * b, 4), "m8", F.Copy)
+            act(("nb", 192 + 33 * b, 224 + 33 * b, 4), "m8", F.Copy, scale=-1.0 / 128)
 
     def own_side(s):
-        ts(low(("xm", 96 + s, 608, 4)), low("modb"), low("rc"), A.is_equal)
+        ts(top(("xm", 98 + s, 608, 4)), top("modb"), top("pr1"), A.is_equal)
 
     def constants_sent():
-        iota("xk", [[0, 512]], 0, 0)
-        iota(("xm", 0, 96, 4), [[128, 3], [0, 8]], 0, 0, 64, 128)
-        iota(("xm", 1, 96, 4), [[0, 3], [16, 8]], 0, 0, 64, 128)
-        iota(("xm", 2, 96, 4), [[0, 24]], 0, 1, 64, 128)
-        iota(("xm", 3, 96, 4), [[0, 24]], 0, 0, 64, 128)
-        iota("fm", [[0, 512]], 0, 0)
-        iota(("mt", 256, 512), [[0, 256]], 0, 0)
-        act(("eb", 4, 516, 4), "idn", F.Copy, scale=0.5)
         act("kh", "kr", F.Copy, bias=0.5)
-        act(("cap", 64, 384), ("one", 0, 320), F.Copy, scale=1e29)
-
-    def constants_travel():
-        act(("cm", 0, 64), ("idn", 0, 64), F.Copy)
-        act(("cm", 64, 68), ("one", 0, 4), F.Copy, scale=0.0)
-        act("uf", "u8", F.Copy)
-        for e in range(4):
-            act(("ut", 512 + e, 1024, 4), ("one", 0, 128), F.Copy, scale=("uf", 4 + e, 5 + e))
-        ts(("cm", 68, 72), ("k24", 0, 4), "p16", A.is_equal)
-        quant(*K, NEG, 128, "ngt", 0)
-        act("gb", "cm", F.Copy, scale=40.0, bias=-40.0)
-        act(("xt", 259, 260), "e0", F.Relu)
-        act(("xt", 2, 288, 4), ("one", 0, 72), F.Copy, scale=16.0)
-        act("vl", "hb", F.Identity, scale=-1.0, bias="bc")
-        act("kb", "k24", F.Copy, scale=16.0, bias=-16.0)
-        act("nkh", "p1", F.Copy, scale=-1.0, bias=0.5)
+        memset(("cap", 64, 384), 1e29)
 
     for t in range(2):
-        c, cs, win, wins = "c%d" % t, "cs%d" % t, "win%d" % t, "wins%d" % t
+        c, cs, wa, was, wb, wbs = ["%s%d" % (x, t) for x in ("c", "cs", "wina", "winas", "winb", "winbs")]
         rep, reps, snd, snds = "rep%d" % t, "reps%d" % t, "snd%d" % t, "snds%d" % t
         nc, ncs = "c%d" % (t + 1), "cs%d" % (t + 1)
-        dma("y", T[win][:, 0:384].bitcast(dt.uint8), T[c][:, 0:384].bitcast(dt.uint8), [whole(c)], [(win, 0, 384)])
-        dma("y", T[wins][:, 0:384], T[cs][:, 0:384], [whole(cs)], [(wins, 0, 384)])
-        dma("y", T[win][:, 448:512].bitcast(dt.uint8), T[c][:, 0:64].bitcast(dt.uint8), [(c, 0, 64)], [(win, 448, 512)])
-        dma("y", T[wins][:, 448:512], T[cs][:, 0:64], [(cs, 0, 64)], [(wins, 448, 512)])
+        for o, os, lo in ((wa, was, 64), (wb, wbs, 0)):
+            dma("y", T[o][:, lo:lo + 384].bitcast(dt.uint8), T[c][:, 0:384].bitcast(dt.uint8), [whole(c)],
+                [(o, lo, lo + 384)])
+            dma("y", T[os][:, lo:lo + 384], T[cs][:, 0:384], [whole(cs)], [(os, lo, lo + 384)])
 
         def against(b, d):
-            o, i = ("mk", 384 * b + 128 * d, 384 * b + 128 * d + 128), ("ps", 512 * (3 + d), 512 * (3 + d) + 128)
+            o, i = ("mk", 384 * b + 128 * d, 384 * b + 128 * d + 128), bank(3 + d, 0, 128)
             if b == d:
                 tt(o, i, ("th", 128 * b, 128 * b + 128), A.is_lt)
             else:
@@ -365,189 +418,176 @@ def rank_program(g, core, T, topo):
             onehot(b)
         ranks = ("scn", 191, 576, 192)
         ts("lv", ranks, 64.0, A.is_lt)
+        act("lw", "lv", F.Copy, scale=2.0)
         quant("xlq", "xls", 0, 128, "xl", 0)
         mm(6, 128, K + (WH,), ("xlq", "xls", 0), True, False)
         mm(6, 128, K + (WL,), ("xlq", "xls", 0), False, True)
         for b in range(3):
-            act(("x1", 384 + 32 * b, 416 + 32 * b, 4), "m8", F.Copy, scale=("lv", b, b + 1))
-        ts(("x1", 320, 332, 4), ranks, 64.0, A.is_lt)
-        act(("x1", 327, 328), ("lv", 0, 1), F.Copy)
-        act(("x1", 331, 332), ("lv", 0, 1), F.Identity, bias=("lv", 1, 2))
-        ts(("x1", 0, 256, 4), ("idn", 0, 64), ("lv", 0, 1), A.mult, 512.0, A.mult)
-        act("lvs", "lv", F.Copy, scale=1.0 / 1024)
+            ts(("x1", 384 + 32 * b, 416 + 32 * b, 4), "m8", ("scn", 192 * b + 191, 192 * b + 192), A.is_gt, -512.0, A.mult)
+            ts(("x1", 320 + 5 * b, 332, 4), ("scn", 191, 576 - 192 * b, 192), 64.0, A.is_lt)
+        ts(("x1", 0, 256, 4), "idn", ("scn", 191, 192), A.is_gt, 512.0, A.mult)
         if t == 0:
             constants_gap()
             constants_nb()
-        run("v", lambda: g.vector.transpose(T.tt[:], T.ps[:, 3072:3200]), [("ps", 3072, 3200)], [whole("tt")])
+        turn("tt", bank(6, 0, 128))
         quant("x1q", "x1s", 0, 128, "x1", 0)
         cp("ofl", ("tt", 0, 128, 32))
         if t == 0:
-            ts("hb", "bc", C32, A.add, C32, A.subtract)
             ts("tl", ("pj", 0, 64), 0.0, A.is_ge)
         pick(snd, snds, 0, 64, c, cs, 384, "ofl", 0)
-        dst = T.cores[rank ^ (1 << t)]
-        rid, pid, _ = topo.addr(dst)
-        m = topo.mask(core, dst)
-        ne = len(topo.engines(core, dst))
-        arr = "arr%d" % t
-        for o, s in ((win, snd), (wins, snds)):
-            dep("p", [whole(s)], [])
-            w, i = T[o][:, 384:448], T[s][:, 0:64]
-            if o == win:
-                w, i = w.bitcast(dt.uint8), i.bitcast(dt.uint8)
-            g.remote_dma(w, i, T.sem[arr], T.sem["loc"], pid, rid, m)
-            count["loc"] += ne
-        count[arr] = 2 * ne
-        clock[(arr, 2 * ne)] = {arr: 2 * ne}
-        for o in (win, wins):
-            hist.setdefault(o, []).append((384, 448, 1, "-", True, arr, 2 * ne))
+        send(t, wa, snd, True)
+        send(t, was, snds, False)
         if t == 0:
             quant(*K, W16, 128, "w16", 0)
-            memset("xt", 0.0)
             constants_sent()
         else:
             quant("wq", "ws", 0, 128, "wt", 0)
         mm(7, 128, K + (ONES,), ("x1q", "x1s", 0))
         mm(0, 128, K + (W16,), ("x1q", "x1s", 0))
-        red("n0", ("ps", 3584, 3649), A.min)
+        if t == 0:
+            quant(*K, EB, 128, "eb", 4)
+        red("n0", bank(7, 0, 65), A.min)
         if t == 0:
             own_side(0)
             own_side(1)
-        ts("ofr", ("ps", 96, 120), "n0", A.max)
-        if t == 0:
-            own_side(2)
-            own_side(3)
+        ts("ofr", bank(0, 96, 120), "n0", A.max)
         pick(rep, reps, 0, 384, c, cs, 384, "ofr", 0)
         mm(6, 128, K + (TRS,), ("x1q", "x1s", 0))
+        if t == 0:
+            for b in range(1, 4):
+                quant(*K, EB + 128 * b, 128, "eb", 4 - b)
         ts(("cap", 0, 64), "kh", "n0", A.subtract, 1e27, A.mult)
         if t == 0:
-            memset(("zr", 3, 4), -1e29)
-            memset(("zr", 388, 404), 1e29)
-            constants_travel()
+            memset(("zr", 0, 8), -1e29)
             dma("y", T.wt[:], T.w[:], [], [whole("wt")])
         else:
             mm(5, 384, ("wq", "ws", 0), (c, cs, 0))
-            act(("yw", 0, 384), ("ps", 2560, 2944), F.Copy)
-        mm(1, 384, (win, wins, 384), (rep, reps, 0))
+            act(("yw", 64, 448), bank(5, 0, 384), F.Copy)
+        mm(1, 384, (wa, was, 0), (rep, reps, 0))
         for b in range(3):
-            ts(("xk", b, 256, 4), "kr", ("ps", 3152 + b, 3153 + b), A.is_equal, ("lvs", b, b + 1), A.mult)
-        quant("xkq", "xks", 0, 128, "xk", 0)
+            ts(("xk", 256 + b, 512, 4), "kr", bank(6, 80 + b, 81 + b), A.is_equal, ("lv", b, b + 1), A.mult)
+            ts(("xk", 512 + b, 1024, 4), "lli", bank(6, 80 + b, 81 + b), A.is_equal, ("lw", b, b + 1), A.mult)
+        quant("xkq", "xks", 0, 256, "xk", 0)
+        mm(5, 128, K + (WH,), ("xkq", "xks", 128), True, False)
+        mm(5, 128, K + (WL,), ("xkq", "xks", 128), False, True)
+        turn("tt", bank(5, 0, 128))
         if t == 0:
             quant(*K, NB, 128, "nb", 0)
-            quant("uq", "us", 128, 128, "ut", 512)
+            ts("cm", ("k24", 0, 4), "p16", A.is_equal)
+            for a in range(2):
+                ts(rows("msk", 32 * a, 32 * a + 32), rows(("pj", 32 * a, 32 * a + 32), 32 * a, 32 * a + 32),
+                   0.0, A.is_le, 1000.0, A.mult)
+            act("gb", "cm", F.Copy, scale=40.0 - 23.0 / 32, bias=-40.0)
+            memset(("xt", 2, 16, 4), 16.0)
+            memset(("xt", 3, 16, 4), 0.0)
         mm(7, 128, ("xkq", "xks", 0), K + (W16,))
         mm(0, 128, ("xkq", "xks", 0), K + (NB,))
         mm(6, 128, K + (WH,), ("xkq", "xks", 0), True, False)
         mm(6, 128, K + (WL,), ("xkq", "xks", 0), False, True)
-
-        def arrived(b):
-            if t == 0:
-                quant(*K, EB + 128 * b, 128, "eb", 4 - b)
-            mm(2 + b, 128, K + (EB + 128 * b,), (win, wins, 384), True, False)
-
-        if t == 1:
-            for b in range(4):
-                arrived(b)
+        for b in range(4):
+            mm(2 + b, 128, K + (EB + 128 * b,), (wa, was, 0), True, False)
 
         def left_side(e):
-            act(("af", e, 512, 4), ("ps", 3584, 3712), F.Copy, scale=1024.0)
+            act(low(("xm", 96 + e, 608, 4)), low(bank(7, 0, 128)), F.Copy)
 
-        scan(("zr", 4, 388), ("ps", 512, 896), "cap", -1e29, A.max, A.min)
+        scan(("zr", 8, 392), bank(1, 0, 384), "cap", -1e29, A.max, A.min)
         left_side(0)
         left_side(1)
-        act("jk", ("zr", 3, 404), F.Sign, bias=("zr", 387, 388), scale=-1.0, acc="ix")
-        if t == 0:
-            arrived(0)
+        act("jk", "zr", F.Sign, bias=("zr", 391, 392), scale=-1.0, acc="ix")
         runs = ("mk", 0, 12)
-        ts(runs, ("zr", 35, 388, 32), ("zr", 387, 388), A.is_lt)
-        if t == 0:
-            arrived(1)
+        ts(runs, ("zr", 39, 392, 32), ("zr", 391, 392), A.is_lt)
         red("i32", runs, A.add)
-        if t == 0:
-            arrived(2)
+        act(top("tab"), top(bank(6, 64, 128)), F.Copy)
         ts("gt", "gb", "i32", A.subtract, 32.0, A.mult)
-        ts(("xt", 0, 288, 4), "cm", "i32", A.mult, 32.0, A.mult)
-        tt("tab", ("ps", 3072, 3136), "kr", A.add)
-        if t == 0:
-            act("bf", "one", F.Copy, scale=0.0)
+        ts(("xt", 0, 16, 4), "cm", "i32", A.mult, 32.0, A.mult)
+        act("v0", "ix", F.Identity, scale=-1.0, bias="bc")
+        act("y2", "ix", F.Copy, scale=(1 + 2.0 ** -10) / 16, bias=C16)
+        act("v1", "v0", F.Copy, bias=C32)
+        act("t16", "y2", F.Copy, scale=16.0, bias=-16.0 * C16)
+        act("vh", "v1", F.Copy, bias=-C32)
+        act("vw", "vh", F.Identity, scale=-1.0, bias="v0")
         left_side(2)
         left_side(3)
-        act("s0", "i32", F.Identity, scale=-32.0, bias="hb")
-        act("a32", "i32", F.Copy, scale=32.0)
-        act("s2", "ix", F.Identity, scale=-1.0, bias="a32")
-        act("ix16", "ix", F.Copy, bias=16.0)
-        ts(("xt", 1, 288, 4), "gt", "ix", A.add, -16.0, A.max)
-        ts("y1", "ix", 7.5, A.add)
-        quant("xtq", "xts", 0, 128, "xt", 0)
-        mm(6, 128, K + (TRS,), ("xtq", "xts", 0), True, False)
-        mm(6, 128, ("xtq", "xts", 0), K + (NEG,), False, True)
-        mm(1, 128, K + (W16,), ("xtq", "xts", 0))
-        ts("t16", "y1", 16.0 * C16, A.add, 16.0 * C16 + 16.0, A.subtract)
         if t == 0:
-            arrived(3)
-        else:
-            quant("afq", "afs", 0, 128, "af", 0)
-        for e in range(4):
-            ts(top(("xm", 96 + e, 608, 4)), top("modb"), top("t16"), A.add, top("ix"), A.is_equal)
-        least("nd", ("ps", 3072, 3137))
-        ts("oft", ("ps", 580, 584), -1.0, A.add)
-        ts(("fm", 0, 256, 4), "tl", "nd", A.is_gt)
+            act("ska", "p16", F.Copy, scale=-32.0, bias=192.0)
+            act("skb", "pr1", F.Copy, scale=-2.0, bias=2.0)
+            act("nk", "kc", F.Copy, scale=-1.0, bias=16.5)
+        act(low(("xm", 0, 96, 2)), low(bank(0, 0, 48)), F.Copy, wr=[low(("xm", 0, 96, 4)), low(("xm", 2, 96, 4))])
+        act(low(("xm", 1, 96, 4)), low(bank(0, 48, 72)), F.Copy, scale=low("ska"))
+        act(low(("xm", 3, 96, 4)), low(bank(0, 48, 72)), F.Copy, scale=low("skb"))
+        if t == 1:
+            mm(0, 128, ("wq", "ws", 0), (wa, was, 0))
+            act(("yw", 0, 64), bank(0, 0, 64), F.Copy)
+        act(top(("tin", 0, 32)), top("msk"), F.Identity, bias=top("ix"))
+        act(rows(("tin", 32, 64), 32, 64), rows(("one", 0, 32), 0, 32), F.Copy, scale=rows("ix", 0, 32))
+        ts(("xt", 1, 16, 4), "gt", "ix", A.add, -16.0, A.max)
+        turn(top("tou"), top("tin"))
+        quant("xtq", "xts", 0, 128, "xt", 0)
+        mm(1, 128, K + (W16,), ("xtq", "xts", 0))
+        ts(top("ne"), top("tou"), top("ix"), A.not_equal)
+        red(top("nd"), top("ne"), A.min)
+        ts(top(("fm", 0, 256, 4)), top("tl"), top("nd"), A.is_gt)
         quant("fmq", "fms", 0, 128, "fm", 0)
-        for b in (6, 7):
+        for b in (0, 7):
             mm(b, 128, K + (ONES,), ("fmq", "fms", 0))
-        for e, x in ((0, "s0"), (1, "vl"), (2, "s2"), (3, -15.0)):
-            act(("nm", e, e + 1), "nd", F.Copy, scale=x)
+        ts("oft", bank(1, 0, 4), -1.0, A.add)
         pick(rep, reps, 0, 64, c, cs, 384, "oft", 0)
-        for e in range(4):
-            ts(top(("xm", e, 96, 4)), top("kb"), top("t16"), A.is_equal, top(("nm", e, e + 1)), A.mult)
         for b in range(4):
             mm(2 + b, 128, K + (EB + 128 * b,), (rep, reps, 0), False, True)
-        act(("jk", 0, 32), ("ps", 3072, 3104), F.Sign, bias="nkh", acc="sa")
-        act(("jk", 32, 64), ("ps", 3104, 3136), F.Sign, bias="nkh", acc="sb")
-        if t == 0:
-            quant("afq", "afs", 0, 128, "af", 0)
-        ts("fl", ("ps", 3647, 3648), "p1", A.is_ge)
-        mm(7, 128, ("fmq", "fms", 0), K + (ONES,))
-        for b in range(4):
-            act(("mt", b, 256, 4), ("ps", 512 * (2 + b), 512 * (2 + b) + 64), F.Copy)
-        act("qa", "nd", F.Copy, scale="ix16", bias=-1.0)
-        act("qb", "nd", F.Copy, scale=1024.0, bias=-1024.0)
+            act(("mt", b, 256, 4), bank(2 + b, 0, 64), F.Copy, scale=0.5)
+        act(top("ixn"), top("nd"), F.Copy, scale=top("ix"))
+        for e in range(2):
+            ts(top(("xm", 96 + e, 608, 4)), top("mod9"), top("t16"), A.add, top("ixn"), A.is_equal)
+        for i in range(4):
+            act(("jk", 64 * i, 64 * i + 64), bank(0, 0, 64), F.Sign, bias=("nk", i, i + 1), acc=("ac", i, i + 1))
+        mm(1, 128, ("fmq", "fms", 0), K + (NB,))
+        for e, x in ((0, "vh"), (1, "vw")):
+            ts(top(("xm", e, 96, 4)), top("kb"), top("t16"), A.is_equal, top(x), A.mult)
+        ts("fl", "nk", bank(7, 63, 64), A.add, 0.0, A.is_lt)
+        tt("ff", "fl", ("tt", 0, 128, 32), A.mult)
         quant("xmq", "xms", 0, 152, "xm", 0)
-        mm(1, 128, ("xmq", "xms", 24), ("xmq", "xms", 0), True, False)
-        run("v", lambda: g.vector.tensor_scalar(T.bf[:, 0:96:2], T.ps[:, 0:48], T.fl[:], None, A.mult),
-            [("ps", 0, 48), whole("fl")], [("bf", 0, 96, 4), ("bf", 2, 96, 4)])
-        ts(("bf", 1, 96, 4), ("ps", 48, 72), "sa", A.mult, "fl", A.mult)
-        ts(("bf", 3, 96, 4), ("ps", 48, 72), "sb", A.mult, "fl", A.mult)
-        quant("bfq", "bfs", 0, 128, "bf", 0)
-        mm(1, 128, ("afq", "afs", 0), ("bfq", "bfs", 0), False, True)
-        ts("xx", "tab", ("ps", 3584, 3585), A.subtract, 1.0, A.add)
-        quant(win, wins, 448, 128, "mt", 0)
-        least("pl", "xx")
-        cp("ofs", ("ps", 512, 536))
-        ts(("tgs", t, t + 1), "pl", "qb", A.mult, "qa", A.add)
+        tt("al", "ac", "ff", A.subtract)
+        ts("ofa", "al", -0.5, A.mult, 32.0, A.add)
+        mm(6, 128, ("xmq", "xms", 24), ("xmq", "xms", 0))
+        act(top("qb"), top("nd"), F.Copy, bias=-1.0)
+        act(top("qa"), top("nd"), F.Identity, scale=-8.0, bias=top("ixn"))
+        pick(wb, wbs, 384, 64, wa, was, 448, "ofa", 0)
+        quant(wb, wbs, 448, 128, "mt", 0)
+        cp("ofs", bank(6, 0, 24))
+
+        def tags():
+            ts(top("xx"), top("tab"), top(bank(1, 80, 81)), A.subtract, 1025.0, A.add)
+            least(top("pl"), top("xx"))
+            ts(top(("tgs", t, t + 1)), top("pl"), top("qb"), A.mult, top("qa"), A.add)
+            dma(None, T.tg[t, :], T.tgs[0:64, t:t + 1], [("tgs", t, t + 1)], [])
+
         if t == 0:
-            dma("y", T.tg[0, :], T.tgs[0:64, 0:1], [("tgs", 0, 1)], [])
+            for e in range(4):
+                ts(("ut", 512 + e, 1024, 4), one128, ("u8", 4 + e, 5 + e), A.mult)
+            quant("uq", "us", 128, 128, "ut", 512)
+            tags()
             for b in range(3):
-                pick(nc, ncs, 128 * b, 128, win, wins, 512, "ofs", 8 * b)
+                pick(nc, ncs, 128 * b, 128, wb, wbs, 512, "ofs", 8 * b)
                 scores(1, b)
         else:
-            mm(2, 128, ("wq", "ws", 0), (win, wins, 384))
-            act(("yw", 384, 512), ("ps", 1024, 1152), F.Copy)
-            pick_rows(ncs, 0, 192, wins, 512, "ofs", 0)
-            pick_rows("ysb", 192, 192, "yw", 512, "ofs", 12)
-            pick_rows(ncs, 192, 192, wins, 512, "ofs", 12)
+            tags()
+            mm(2, 128, ("wq", "ws", 0), (wb, wbs, 448))
+            pick_rows("yw", 448, 64, "yw", 448, "ofa", 0)
+            act(("yw", 512, 576), bank(2, 0, 64), F.Copy)
+            pick_rows(ncs, 0, 192, wbs, 512, "ofs", 0)
+            pick_rows("ysb", 192, 192, "yw", 512, "ofs", 12, 64)
+            pick_rows(ncs, 192, 192, wbs, 512, "ofs", 12)
             for b in range(2):
-                pick_codes(nc, 192 * b, 192, win, 512, "ofs", 12 * b)
-                dma("y", T.oc[:, 768 * b:768 * b + 768], T[nc][:, 192 * b:192 * b + 192].bitcast(dt.uint8),
+                pick_codes(nc, 192 * b, 192, wb, 512, "ofs", 12 * b)
+                dma(None, T.oc[:, 768 * b:768 * b + 768], T[nc][:, 192 * b:192 * b + 192].bitcast(dt.uint8),
                     [(nc, 192 * b, 192 * b + 192)], [])
-                if b == 0:
-                    dma("y", T.tg[1, :], T.tgs[0:64, 1:2], [("tgs", 1, 2)], [])
-                    dma("y", T.y[:, 192:384], T.ysb[:, 192:384], [("ysb", 192, 384)], [])
-            run("v", lambda: g.vector.tensor_copy(T.ysb[:, 0:192], T.yw[:].indirect(T.ofs[:, 0:12])),
-                [whole("yw"), ("ofs", 0, 12)], [("ysb", 0, 192)])
+            dma(None, T.y[:, 192:384], T.ysb[:, 192:384], [("ysb", 192, 384)], [])
+            pick_rows("ysb", 0, 192, "yw", 512, "ofs", 0, 64)
             for k in range(4):
-                dma("s", T.osc[4 * k:4 * k + 4, :], T[ncs][32 * k:32 * k + 4, 0:384], [whole(ncs)], [])
-            dma("y", T.y[:, 0:192], T.ysb[:, 0:192], [("ysb", 0, 192)], [])
+                dma(None, T.osc[4 * k:4 * k + 4, :], T[ncs][32 * k:32 * k + 4, 0:384], [whole(ncs)], [])
+            dma(None, T.y[:, 0:192], T.ysb[:, 0:192], [("ysb", 0, 192)], [])
+    for i in (ORDER.split() if ORDER else range(len(calls))):
+        calls[int(i)][1]()
     for s in SEMAPHORES:
         if count[s]:
             g.wait_ge(T.sem[s], count[s])

from concourse.mybir import dt, AluOpType as A, AxisListType, ActivationFunctionType as F

F8, U8, BF, F32, U16 = "float8_e4m3fn_x4", "uint8", "bfloat16", "float32", "uint16"
C16 = 12582912.0
C32 = 402653184.0
SCRATCH = {"ps": ("psum", [128, 4096], F32)}
for _t, _l in (
        (BF, "ct 1536 u8 8 ut 1024 wt 512 modb 128 lli 128 xo 536 eb 520 mw 768 ft 1536 "
             "tri 128 idn 64 m8 8 cm 4 kb 24 kr 64 mk 1152 scn 576 xl 512 x1 512 cap 384 jk 392 "
             "gb 4 nb 512 tl 64 xm 608 ne 64 whl 1024 h16 80 mod9 128"),
        (F32, "pj 128 p1 1 k24 24 jb 4 h4 4 l4 4 yy 1 p16 1 pr1 1 bc 1 sc 3 sd 3 "
              "th 384 tt 128 lv 3 lw 3 n0 1 kh 64 zr 392 ix 1 i32 1 y2 1 t16 1 xx 64 tab 64 pl 1 qa 1 qb 1 "
              "tgs 2 ysb 384 yw 576 hn 4 l5 4 nd 1 v0 1 v1 1 vh 1 vw 1 ixn 1 msk 32 tin 64 tou 64 "
              "ska 1 skb 1 kc 4 nk 4 ac 4 fl 4 ff 4 al 4 m240 1 gt 4"),
        (U16, "ofl 4 ofr 24 oft 4 ofa 4 ofs 24"),
        (F8, "uq 256 wq 128 kq 1408 xlq 128 x1q 128 xkq 256 xtq 128 fmq 128 xmq 152 c0 384 c1 384 "
             "c2 384 wina0 448 wina1 448 winb0 576 winb1 576 rep0 384 rep1 384 snd0 64 snd1 64"),
        (U8, "us 256 ws 128 ks 1408 xls 128 x1s 128 xks 256 xts 128 fms 128 xms 152 cs0 384 cs1 384 "
             "cs2 384 winas0 448 winas1 448 winbs0 576 winbs1 576 reps0 384 reps1 384 snds0 64 snds1 64")):
    _w = _l.split()
    for _n, _c in zip(_w[::2], _w[1::2]):
        SCRATCH[_n] = ("sbuf", [128, int(_c)], _t)
NDMA = 24
SEMAPHORES = ["sv", "ss", "st", "sp", "loc", "arr0", "arr1"] + ["d%d" % i for i in range(NDMA)]
ONES, W16, TRS, WH, WL, EB, NB = 0, 128, 256, 384, 512, 640, 1280
PARTS = {"xt": ("xo", 0, 16), "one": ("xo", 16, 536), "fm": ("ft", 0, 256), "trs": ("ft", 256, 768),
         "xk": ("ft", 512, 1536), "mt": ("mw", 0, 256), "w16": ("mw", 256, 768)}
SMALL = [_n for _n, _v in SCRATCH.items() if _v[2] == F32 and _v[1][1] <= 4 and _n != "tgs"]
SCRATCH["sm"] = ("sbuf", [128, 4 * len(SMALL)], F32)
for _i, _n in enumerate(SMALL):
    PARTS[_n] = ("sm", 4 * _i, 4 * _i + SCRATCH.pop(_n)[1][1])
QUEUES = "ssvsssssvsssssssssssssssssvssssssssssssssssssssssssssssssssssssssssssssssssssvvsssssvssssvsssvssssssssssvssvsvssssssvssvsvvsssssvvssvssvvvsvssvv"
ORDER = """12 5 0 23 49 1 4 2 3 6 35 47 34 13 15 39 71 155 38 37 9 169 53 36 41 251 58 55 56 40 42 48 44 57 46 60 8 16 7 59 250 63 252 28 45 43 70 168 139 27 61 64 65 62 77 66 69 79 78 81 91 92 95 80 173 67 68 82 94 93 97 83 74 76 73 84 98 72 85 21 96 99 101 100 102 89 30 104 172 52 18 128 20 103 88 122 14 19 154 105 132 108 112 115 54 109 111 106 110 114 26 129 17 11 10 24 127 120 124 116 131 113 75 133 145 117 90 86 22 87 135 200 171 25 107 134 138 123 51 119 130 140 149 137 150 142 31 143 162 160 141 146 157 161 136 158 147 29 32 118 33 121 199 153 125 126 201 148 159 151 156 50 163 182 174 197 185 167 186 170 144 180 176 179 206 187 152 189 175 202 192 183 164 165 190 205 207 203 191 208 177 209 178 211 166 198 212 193 210 181 204 213 194 195 217 228 184 196 214 218 219 188 230 215 216 229 236 237 231 253 222 224 220 233 238 240 226 239 232 234 254 241 243 225 221 223 235 227 242 249 248 247 260 246 264 255 259 263 261 267 265 266 256 268 275 271 274 318 270 269 284 262 277 276 278 280 286 281 287 285 282 279 290 289 283 245 291 244 288 292 294 327 293 295 297 296 298 306 301 272 309 273 302 299 307 305 304 308 310 303 311 312 319 313 257 314 328 300 325 320 321 334 322 335 316 315 317 333 324 330 323 332 331 329 326 336 340 341 345 348 337 338 346 342 350 367 352 353 363 339 343 347 365 351 355 356 370 344 371 357 372 373 374 359 366 364 376 375 361 349 358 377 360 368 378 382 393 369 379 380 362 383 381 384 395 394 391 389 354 402 401 398 399 397 396 385 403 405 387 400 404 386 392 390 258 408 409 410 388 406 415 413 407 419 414 416 420 421 411 417 423 418 427 412 430 425 428 422 429 435 426 424 431 433 432 434"""


def rank_program(g, core, T, topo):
    rank = T.rank_of(core)
    if rank is None:
        return
    queue = {"v": g.vector, "s": g.scalar, "t": g.tensor, "p": g, "y": g.sync}
    own = {"v": "sv", "s": "ss", "t": "st", "p": "sp"}
    count = {s: 0 for s in SEMAPHORES}
    clock = {}
    known = {q: {} for q in queue}
    hist = {}
    ndma = [0]
    turns = [0]
    calls = []

    def merge(a, b):
        for s, v in b.items():
            if a.get(s, 0) < v:
                a[s] = v

    def span(reg):
        if reg[0] == "ps":
            return reg[1] // 512 * 512, (reg[2] + 511) // 512 * 512, 1, 0, 128
        return (reg[1], reg[2], reg[3] if len(reg) > 3 else 1) + (tuple(reg[4:]) or (0, 128))

    def dep(q, rd, wr):
        need = {}
        for lst, w in ((rd, False), (wr, True)):
            for reg in lst:
                psum = reg[0] == "ps"
                lo, hi, st, p0, p1 = span(reg)
                for (l2, h2, s2, p2, p3, q2, w2, sem, val) in hist.get(reg[0], ()):
                    if l2 >= hi or lo >= h2 or p2 >= p1 or p0 >= p3 or (st == s2 and st > 1 and (lo - l2) % st):
                        continue
                    if psum and q == q2 and (q == "t" or not (w or w2)):
                        continue
                    if w or w2 or (psum and q != q2):
                        need[sem] = max(need.get(sem, 0), val)
        for sem in sorted(need, key=lambda s: s == own.get(q)):
            if known[q].get(sem, 0) < need[sem]:
                queue[q].wait_ge(T.sem[sem], need[sem])
                merge(known[q], clock[(sem, need[sem])])

    def note(q, rd, wr, sem, val):
        c = dict(known[q])
        c[sem] = val
        if (sem, val - 1) in clock:
            merge(c, clock[(sem, val - 1)])
        clock[(sem, val)] = c
        for lst, w in ((rd, False), (wr, True)):
            for reg in lst:
                hist.setdefault(reg[0], []).append(span(reg) + (q, w, sem, val))

    def view(reg):
        name, lo, hi = reg[0], reg[1], reg[2]
        if len(reg) > 4:
            return T[name][reg[4]:reg[5], lo:hi:reg[3]]
        return T[name][:, lo:hi:reg[3]] if len(reg) > 3 else T[name][:, lo:hi]

    def run(q, call, rd, wr):
        def issue():
            dep(q, rd, wr)
            sem = own[q]
            count[sem] += 1
            call().then_inc(T.sem[sem], 1)
            note(q, rd, wr, sem, count[sem])
        calls.append((q, issue, rd, wr))

    def whole(name):
        return PARTS[name] if name in PARTS else (name, 0, SCRATCH[name][1][1])

    def R(x):
        if isinstance(x, str):
            return whole(x)
        if x[0] in PARTS:
            name, lo, _ = PARTS[x[0]]
            return (name, lo + x[1], lo + x[2]) + tuple(x[3:])
        return x

    def isreg(x):
        return isinstance(x, (str, tuple))

    def rows(x, p0, p1):
        x = R(x)
        return (x[0], x[1], x[2], x[3] if len(x) > 3 else 1, p0, p1)

    def top(x):
        return rows(x, 0, 64)

    def low(x):
        return rows(x, 64, 128)

    def bank(b, lo, hi):
        return ("ps", 512 * b + lo, 512 * b + hi)

    def either():
        turns[0] += 1
        return QUEUES[turns[0] - 1]

    def memset(o, v):
        o = R(o)
        if o != R("one") and either() == "s":
            i = R(("one", 0, len(range(*span(o)[:3])), 1) + span(o)[3:])
            run("s", lambda: g.scalar.activation(view(o), view(i), F.Copy, scale=0.0, bias=v), [i], [o])
        else:
            run("v", lambda: g.vector.memset(view(o), v), [], [o])

    def ts(o, i, s1, op0, s2=None, op1=None, wr=None):
        o, i = R(o), R(i)
        wr = wr or [o]
        rd = [i] + [R(s) for s in (s1, s2) if isreg(s)]
        a = view(R(s1)) if isreg(s1) else s1
        b = view(R(s2)) if isreg(s2) else s2
        if op1 is None:
            run("v", lambda: g.vector.tensor_scalar(view(o), view(i), a, None, op0), rd, wr)
        else:
            run("v", lambda: g.vector.tensor_scalar(view(o), view(i), a, b, op0, op1), rd, wr)

    def tt(o, a, b, op):
        o, a, b = R(o), R(a), R(b)
        run("v", lambda: g.vector.tensor_tensor(view(o), view(a), view(b), op), [a, b], [o])

    def cp(o, i):
        o, i = R(o), R(i)
        run("v", lambda: g.vector.tensor_copy(view(o), view(i)), [i], [o])

    def red(o, i, op):
        o, i = R(o), R(i)
        run("v", lambda: g.vector.tensor_reduce(view(o), view(i), AxisListType.X, op), [i], [o])

    def least(o, i):
        o, i = R(o), R(i)
        run("v", lambda: g.vector.tensor_reduce(view(o), view(i), AxisListType.X, A.min, apply_absolute_value=True),
            [i], [o])

    def scan(o, a, b, init, op0, op1):
        o, a, b = R(o), R(a), R(b)
        run("v", lambda: g.vector.tensor_tensor_scan(view(o), view(a), view(b), init, op0, op1), [a, b], [o])

    def turn(o, i):
        o, i = R(o), R(i)
        run("v", lambda: g.vector.transpose(view(o), view(i)), [i], [o])

    def act(o, i, func, bias=None, scale=None, acc=None, wr=None):
        o, i = R(o), R(i)
        if func in (F.Copy, F.Identity) and either() == "v":
            if bias is None:
                return ts(o, i, 1.0 if scale is None else scale, A.mult, wr=wr)
            return ts(o, i, 1.0 if scale is None else scale, A.mult, bias, A.add, wr=wr)
        rd, wr, kw = [i], wr or [o], {}
        for k, x in (("bias", bias), ("scale", scale)):
            if isreg(x):
                rd.append(R(x))
                kw[k] = view(R(x))
            elif x is not None:
                kw[k] = x
        if acc is not None:
            wr.append(R(acc))
            kw["accum_out"] = view(R(acc))
        run("s", lambda: g.scalar.activation(view(o), view(i), func, **kw), rd, wr)

    def quant(qn, sn, lo, n, src, slo):
        s = R((src, slo, slo + 4 * n))
        run("v", lambda: g.vector.quantize_mx(T[qn][:, lo:lo + n], T[sn][:, lo:lo + n], view(s)),
            [s], [(qn, lo, lo + n), (sn, lo, lo + n)])

    def mm(b, n, l, r, start=True, stop=True):
        o = bank(b, 0, n)
        rl = [(l[0], l[2], l[2] + 128), (l[1], l[2], l[2] + 128), (r[0], r[2], r[2] + n), (r[1], r[2], r[2] + n)]
        run("t", lambda: g.tensor.matmul_mx(view(o), view(rl[0]), view(rl[1]), view(rl[2]), view(rl[3]), start, stop),
            rl, [o])

    def pick_codes(o, olo, n, win, wide, off, off0):
        k = (off, off0, off0 + n // 16)
        run("v", lambda: g.vector.tensor_copy(T[o][:, olo:olo + n].bitcast(dt.uint32),
                                              T[win][:, 0:wide].bitcast(dt.uint32).indirect(view(k))),
            [(win, 0, wide), k], [(o, olo, olo + n)])

    def pick_rows(o, olo, n, win, wide, off, off0, lo=0):
        q = either()
        k = (off, off0, off0 + n // 16)
        rd, wr = [(win, lo, lo + wide), k], [(o, olo, olo + n)]
        if q == "s":
            run(q, lambda: g.scalar.activation(view(wr[0]), view(rd[0]).indirect(view(k)), F.Copy), rd, wr)
        else:
            run(q, lambda: g.vector.tensor_copy(view(wr[0]), view(rd[0]).indirect(view(k))), rd, wr)

    def pick(o, os, olo, n, win, wins, wide, off, off0):
        pick_codes(o, olo, n, win, wide, off, off0)
        pick_rows(os, olo, n, wins, wide, off, off0)

    def iota(o, pattern, base, cm):
        o = R(o)
        run("p", lambda: g.iota(view(o), pattern, base, cm, allow_small_or_imprecise_dtypes=True), [], [o])

    def select(o, pattern, op, base, cm):
        o = R(o)
        i = R(("one", 0, len(range(*span(o)[:3]))))
        run("p", lambda: g.affine_select(view(o), view(i), pattern, op, 0.0, base, cm), [i], [o])

    def dma(q, out, in_, rd, wr):
        q = q or ("s" if either() == "s" else "y")

        def issue():
            dep(q, rd, wr)
            sem = "d%d" % ndma[0]
            ndma[0] += 1
            count[sem] = 16
            queue[q].dma_start(out, in_).then_inc(T.sem[sem], 16)
            note(q, rd, wr, sem, 16)
        calls.append((q, issue, rd, wr))

    def send(t, o, s, codes):
        dst = T.cores[rank ^ (1 << t)]
        rid, pid, _ = topo.addr(dst)
        ne = len(topo.engines(core, dst))
        arr = "arr%d" % t

        def issue():
            dep("p", [whole(s)], [])
            w, i = T[o][:, 0:64], T[s][:, 0:64]
            if codes:
                w, i = w.bitcast(dt.uint8), i.bitcast(dt.uint8)
            g.remote_dma(w, i, T.sem[arr], T.sem["loc"], pid, rid, topo.mask(core, dst))
            count["loc"] += ne
            count[arr] = 2 * ne
            clock[(arr, 2 * ne)] = {arr: 2 * ne}
            hist.setdefault(o, []).append((0, 64, 1, 0, 128, "-", True, arr, 2 * ne))
        calls.append(("p", issue, [whole(s)], [(o, 0, 64)]))

    K = ("kq", "ks")
    one128 = ("one", 0, 128)

    dma("y", T.u8[:], T.u[:, 0:8], [], [whole("u8")])
    dma("s", T.ct[:, 0:512], T.c[:, 0:512], [], [("ct", 0, 512)])
    dma("y", T.ct[:, 512:1024], T.c[:, 512:1024], [], [("ct", 512, 1024)])
    dma("s", T.ct[:, 1024:1536], T.c[:, 1024:1536], [], [("ct", 1024, 1536)])

    iota("jb", [[128, 4]], 0, 1)
    iota("p1", [[0, 1]], 1, 1)
    iota("pj", [[1, 128]], 0, -1)
    iota("lli", [[16, 4], [0, 2], [1, 16]], 0, 0)
    iota("modb", [[0, 8], [1, 16]], 1, 0)
    iota("k24", [[1, 24]], 0, 0)
    iota("kr", [[1, 64]], 0, 0)
    iota("h16", [[16, 5], [0, 16]], 0, 0)
    memset("one", 1.0)
    memset(("xk", 259, 1024, 4), 0.0)
    memset("fm", 0.0)
    memset("x1", 0.0)
    select("eb", [[1, 520]], A.is_equal, -4, -4)
    select(("trs", 0, 512, 4), [[1, 128]], A.is_gt, 0, -1)
    for e in (1, 2, 3):
        memset(("trs", e, 512, 4), 1.0)
    memset(top(("xm", 0, 96)), 0.0)
    memset(rows(("tin", 32, 64), 0, 32), 1000.0)

    def places(x, lo, n, row):
        act(rows((x, lo, lo + 4 * n - 3, 4), 0, 1), rows(("h16", 0, n), 0, 1), F.Copy)
        act(rows((x, lo, lo + 4 * n - 3, 4), row, row + 1), rows(("modb", 0, n), row, row + 1), F.Copy, bias=-1.0)

    def offsets(x, lo):
        ts(rows((x, lo, lo + 95, 4), 0, 16), rows("k24", 0, 16), 16.0, A.mult, 240.0, A.min)
        act(rows((x, lo + 1, lo + 95, 4), 0, 16), rows("k24", 0, 16), F.Relu, scale=16.0, bias=rows("m240", 0, 16))
        act(rows((x, lo, lo + 95, 4), 32, 48), rows(("one", 0, 24), 32, 48), F.Copy, scale=rows("p1", 32, 48), bias=-33.0)

    memset("m240", -240.0)
    places("x1", 1, 80, 32)
    offsets("x1", 385)
    places("xk", 259, 64, 32)
    offsets("xm", 2)
    ts("h4", "jb", C32, A.add, C32, A.subtract)
    act("yy", "p1", F.Copy, scale=0.0625, bias=-8.5 / 16)
    ts("tri", "pj", 0.0, A.is_lt)
    tt("l4", "jb", "h4", A.subtract)
    ts("p16", "yy", C16, A.add, C16, A.subtract)
    for h, x in ((0, "h4"), (1, "l4")):
        for b in range(3):
            act(("whl", 512 * h + b, 512 * h + 512, 4), one128, F.Copy, scale=(x, b, b + 1))
    memset(("whl", 3, 512, 4), 1024.0)
    memset(("whl", 515, 1024, 4), 0.0)
    memset(("w16", 3, 512, 4), 0.0)
    memset(("xl", 3, 512, 4), 0.0)
    memset("nb", 0.0)
    memset(("nb", 320, 321), 1024.0)
    quant(*K, ONES, 128, "one", 0)
    act("pr1", "p16", F.Identity, scale=-16.0, bias="p1")
    ts("idn", ("pj", 0, 64), 0.0, A.is_equal, 64.0, A.mult)
    ts(("w16", 0, 512, 4), "modb", "pr1", A.is_equal)
    for e in range(4):
        ts(("ut", e, 512, 4), one128, ("u8", e, e + 1), A.mult)
    quant("uq", "us", 0, 128, "ut", 0)

    def scores(t, b):
        c, s, u = "c%d" % t, "cs%d" % t, ("uq", "us", 128 * t)
        mm(b, 128, (c, s, 128 * b), u)
        mm(3 + b, 128, u, (c, s, 128 * b))

    def column(b):
        act(("sc", b, b + 1), bank(b, 0, 1), F.Copy)

    def spacing(b):
        act(("sd", b, b + 1), bank(b, 0, 1), F.Abs, bias=2.0 ** -120, scale=0.6 * 2.0 ** -23)

    def threshold(b):
        act(("th", 128 * b, 128 * b + 128), "tri", F.Identity, bias=("sc", b, b + 1), scale=("sd", b, b + 1))

    for b in range(3):
        quant("c0", "cs0", 128 * b, 128, "ct", 512 * b)
        scores(0, b)
    quant(*K, WH, 256, "whl", 0)
    ts("m8", ("k24", 0, 8), "p16", A.is_equal, 64.0, A.mult)
    act("hn", "h4", F.Copy, scale=-1.0 / 64, bias=6.5)
    act("l5", "l4", F.Copy, scale=-1.0 / 64)

    def constants_ranks():
        for i in range(2):
            act(("w16", i + 1, 512, 4), ("w16", 0, 512, 4), F.Copy)
        act("kb", "k24", F.Copy, scale=16.0, bias=16.0)
        act("mod9", "modb", F.Copy, bias=-9.0)
        act("kc", ("kb", 0, 4), F.Identity, bias="pr1")

    def constants_gap():
        act("bc", "p1", F.Copy, bias=455.0)
        quant(*K, TRS, 128, "trs", 0)

    def constants_nb():
        for b in range(3):
            act(("nb", 65 * b, 65 * b + 64, 8), "m8", F.Copy, scale=("hn", b, b + 1))
            act(("nb", 65 * b + 4, 65 * b + 64, 8), "m8", F.Copy, scale=("l5", b, b + 1))
            act(("nb", 192 + 33 * b, 224 + 33 * b, 4), "m8", F.Copy, scale=-1.0 / 128)

    def own_side(s):
        ts(top(("xm", 98 + s, 608, 4)), top("modb"), top("pr1"), A.is_equal)

    def constants_sent():
        act("kh", "kr", F.Copy, bias=0.5)
        memset(("cap", 64, 384), 1e29)

    for t in range(2):
        c, cs, wa, was, wb, wbs = ["%s%d" % (x, t) for x in ("c", "cs", "wina", "winas", "winb", "winbs")]
        rep, reps, snd, snds = "rep%d" % t, "reps%d" % t, "snd%d" % t, "snds%d" % t
        nc, ncs = "c%d" % (t + 1), "cs%d" % (t + 1)
        for o, os, lo in ((wa, was, 64), (wb, wbs, 0)):
            dma("y", T[o][:, lo:lo + 384].bitcast(dt.uint8), T[c][:, 0:384].bitcast(dt.uint8), [whole(c)],
                [(o, lo, lo + 384)])
            dma("y", T[os][:, lo:lo + 384], T[cs][:, 0:384], [whole(cs)], [(os, lo, lo + 384)])

        def against(b, d):
            o, i = ("mk", 384 * b + 128 * d, 384 * b + 128 * d + 128), bank(3 + d, 0, 128)
            if b == d:
                tt(o, i, ("th", 128 * b, 128 * b + 128), A.is_lt)
            else:
                ts(o, i, ("sc", b, b + 1), A.is_le if d < b else A.is_lt)

        def total(b):
            scan(("scn", 192 * b, 192 * b + 192), ("mk", 384 * b, 384 * b + 192), ("mk", 384 * b + 192, 384 * b + 384),
                 0.0, A.add, A.add)

        def onehot(b):
            ts(("xl", b, 512, 4), "lli", ("scn", 192 * b + 191, 192 * b + 192), A.is_equal)

        column(0)
        if t == 0:
            column(1)
            spacing(0)
            spacing(1)
        else:
            spacing(0)
            column(1)
            spacing(1)
        threshold(0)
        column(2)
        spacing(2)
        threshold(1)
        threshold(2)
        if t == 0:
            constants_ranks()
        for b, d in ((0, 1), (1, 0), (0, 2), (1, 2), (0, 0), (2, 0), (2, 1), (1, 1), (2, 2)):
            against(b, d)
        for b in range(3):
            total(b)
        for b in range(3):
            onehot(b)
        ranks = ("scn", 191, 576, 192)
        ts("lv", ranks, 64.0, A.is_lt)
        act("lw", "lv", F.Copy, scale=2.0)
        quant("xlq", "xls", 0, 128, "xl", 0)
        mm(6, 128, K + (WH,), ("xlq", "xls", 0), True, False)
        mm(6, 128, K + (WL,), ("xlq", "xls", 0), False, True)
        for b in range(3):
            ts(("x1", 384 + 32 * b, 416 + 32 * b, 4), "m8", ("scn", 192 * b + 191, 192 * b + 192), A.is_gt, -512.0, A.mult)
            ts(("x1", 320 + 5 * b, 332, 4), ("scn", 191, 576 - 192 * b, 192), 64.0, A.is_lt)
        ts(("x1", 0, 256, 4), "idn", ("scn", 191, 192), A.is_gt, 512.0, A.mult)
        if t == 0:
            constants_gap()
            constants_nb()
        turn("tt", bank(6, 0, 128))
        quant("x1q", "x1s", 0, 128, "x1", 0)
        cp("ofl", ("tt", 0, 128, 32))
        if t == 0:
            ts("tl", ("pj", 0, 64), 0.0, A.is_ge)
        pick(snd, snds, 0, 64, c, cs, 384, "ofl", 0)
        send(t, wa, snd, True)
        send(t, was, snds, False)
        if t == 0:
            quant(*K, W16, 128, "w16", 0)
            constants_sent()
        else:
            quant("wq", "ws", 0, 128, "wt", 0)
        mm(7, 128, K + (ONES,), ("x1q", "x1s", 0))
        mm(0, 128, K + (W16,), ("x1q", "x1s", 0))
        if t == 0:
            quant(*K, EB, 128, "eb", 4)
        red("n0", bank(7, 0, 65), A.min)
        if t == 0:
            own_side(0)
            own_side(1)
        ts("ofr", bank(0, 96, 120), "n0", A.max)
        pick(rep, reps, 0, 384, c, cs, 384, "ofr", 0)
        mm(6, 128, K + (TRS,), ("x1q", "x1s", 0))
        if t == 0:
            for b in range(1, 4):
                quant(*K, EB + 128 * b, 128, "eb", 4 - b)
        ts(("cap", 0, 64), "kh", "n0", A.subtract, 1e27, A.mult)
        if t == 0:
            memset(("zr", 0, 8), -1e29)
            dma("y", T.wt[:], T.w[:], [], [whole("wt")])
        else:
            mm(5, 384, ("wq", "ws", 0), (c, cs, 0))
            act(("yw", 64, 448), bank(5, 0, 384), F.Copy)
        mm(1, 384, (wa, was, 0), (rep, reps, 0))
        for b in range(3):
            ts(("xk", 256 + b, 512, 4), "kr", bank(6, 80 + b, 81 + b), A.is_equal, ("lv", b, b + 1), A.mult)
            ts(("xk", 512 + b, 1024, 4), "lli", bank(6, 80 + b, 81 + b), A.is_equal, ("lw", b, b + 1), A.mult)
        quant("xkq", "xks", 0, 256, "xk", 0)
        mm(5, 128, K + (WH,), ("xkq", "xks", 128), True, False)
        mm(5, 128, K + (WL,), ("xkq", "xks", 128), False, True)
        turn("tt", bank(5, 0, 128))
        if t == 0:
            quant(*K, NB, 128, "nb", 0)
            ts("cm", ("k24", 0, 4), "p16", A.is_equal)
            for a in range(2):
                ts(rows("msk", 32 * a, 32 * a + 32), rows(("pj", 32 * a, 32 * a + 32), 32 * a, 32 * a + 32),
                   0.0, A.is_le, 1000.0, A.mult)
            act("gb", "cm", F.Copy, scale=40.0 - 23.0 / 32, bias=-40.0)
            memset(("xt", 2, 16, 4), 16.0)
            memset(("xt", 3, 16, 4), 0.0)
        mm(7, 128, ("xkq", "xks", 0), K + (W16,))
        mm(0, 128, ("xkq", "xks", 0), K + (NB,))
        mm(6, 128, K + (WH,), ("xkq", "xks", 0), True, False)
        mm(6, 128, K + (WL,), ("xkq", "xks", 0), False, True)
        for b in range(4):
            mm(2 + b, 128, K + (EB + 128 * b,), (wa, was, 0), True, False)

        def left_side(e):
            act(low(("xm", 96 + e, 608, 4)), low(bank(7, 0, 128)), F.Copy)

        scan(("zr", 8, 392), bank(1, 0, 384), "cap", -1e29, A.max, A.min)
        left_side(0)
        left_side(1)
        act("jk", "zr", F.Sign, bias=("zr", 391, 392), scale=-1.0, acc="ix")
        runs = ("mk", 0, 12)
        ts(runs, ("zr", 39, 392, 32), ("zr", 391, 392), A.is_lt)
        red("i32", runs, A.add)
        act(top("tab"), top(bank(6, 64, 128)), F.Copy)
        ts("gt", "gb", "i32", A.subtract, 32.0, A.mult)
        ts(("xt", 0, 16, 4), "cm", "i32", A.mult, 32.0, A.mult)
        act("v0", "ix", F.Identity, scale=-1.0, bias="bc")
        act("y2", "ix", F.Copy, scale=(1 + 2.0 ** -10) / 16, bias=C16)
        act("v1", "v0", F.Copy, bias=C32)
        act("t16", "y2", F.Copy, scale=16.0, bias=-16.0 * C16)
        act("vh", "v1", F.Copy, bias=-C32)
        act("vw", "vh", F.Identity, scale=-1.0, bias="v0")
        left_side(2)
        left_side(3)
        if t == 0:
            act("ska", "p16", F.Copy, scale=-32.0, bias=192.0)
            act("skb", "pr1", F.Copy, scale=-2.0, bias=2.0)
            act("nk", "kc", F.Copy, scale=-1.0, bias=16.5)
        act(low(("xm", 0, 96, 2)), low(bank(0, 0, 48)), F.Copy, wr=[low(("xm", 0, 96, 4)), low(("xm", 2, 96, 4))])
        act(low(("xm", 1, 96, 4)), low(bank(0, 48, 72)), F.Copy, scale=low("ska"))
        act(low(("xm", 3, 96, 4)), low(bank(0, 48, 72)), F.Copy, scale=low("skb"))
        if t == 1:
            mm(0, 128, ("wq", "ws", 0), (wa, was, 0))
            act(("yw", 0, 64), bank(0, 0, 64), F.Copy)
        act(top(("tin", 0, 32)), top("msk"), F.Identity, bias=top("ix"))
        act(rows(("tin", 32, 64), 32, 64), rows(("one", 0, 32), 0, 32), F.Copy, scale=rows("ix", 0, 32))
        ts(("xt", 1, 16, 4), "gt", "ix", A.add, -16.0, A.max)
        turn(top("tou"), top("tin"))
        quant("xtq", "xts", 0, 128, "xt", 0)
        mm(1, 128, K + (W16,), ("xtq", "xts", 0))
        ts(top("ne"), top("tou"), top("ix"), A.not_equal)
        red(top("nd"), top("ne"), A.min)
        ts(top(("fm", 0, 256, 4)), top("tl"), top("nd"), A.is_gt)
        quant("fmq", "fms", 0, 128, "fm", 0)
        for b in (0, 7):
            mm(b, 128, K + (ONES,), ("fmq", "fms", 0))
        ts("oft", bank(1, 0, 4), -1.0, A.add)
        pick(rep, reps, 0, 64, c, cs, 384, "oft", 0)
        for b in range(4):
            mm(2 + b, 128, K + (EB + 128 * b,), (rep, reps, 0), False, True)
            act(("mt", b, 256, 4), bank(2 + b, 0, 64), F.Copy, scale=0.5)
        act(top("ixn"), top("nd"), F.Copy, scale=top("ix"))
        for e in range(2):
            ts(top(("xm", 96 + e, 608, 4)), top("mod9"), top("t16"), A.add, top("ixn"), A.is_equal)
        for i in range(4):
            act(("jk", 64 * i, 64 * i + 64), bank(0, 0, 64), F.Sign, bias=("nk", i, i + 1), acc=("ac", i, i + 1))
        mm(1, 128, ("fmq", "fms", 0), K + (NB,))
        for e, x in ((0, "vh"), (1, "vw")):
            ts(top(("xm", e, 96, 4)), top("kb"), top("t16"), A.is_equal, top(x), A.mult)
        ts("fl", "nk", bank(7, 63, 64), A.add, 0.0, A.is_lt)
        tt("ff", "fl", ("tt", 0, 128, 32), A.mult)
        quant("xmq", "xms", 0, 152, "xm", 0)
        tt("al", "ac", "ff", A.subtract)
        ts("ofa", "al", -0.5, A.mult, 32.0, A.add)
        mm(6, 128, ("xmq", "xms", 24), ("xmq", "xms", 0))
        act(top("qb"), top("nd"), F.Copy, bias=-1.0)
        act(top("qa"), top("nd"), F.Identity, scale=-8.0, bias=top("ixn"))
        pick(wb, wbs, 384, 64, wa, was, 448, "ofa", 0)
        quant(wb, wbs, 448, 128, "mt", 0)
        cp("ofs", bank(6, 0, 24))

        def tags():
            ts(top("xx"), top("tab"), top(bank(1, 80, 81)), A.subtract, 1025.0, A.add)
            least(top("pl"), top("xx"))
            ts(top(("tgs", t, t + 1)), top("pl"), top("qb"), A.mult, top("qa"), A.add)
            dma(None, T.tg[t, :], T.tgs[0:64, t:t + 1], [("tgs", t, t + 1)], [])

        if t == 0:
            for e in range(4):
                ts(("ut", 512 + e, 1024, 4), one128, ("u8", 4 + e, 5 + e), A.mult)
            quant("uq", "us", 128, 128, "ut", 512)
            tags()
            for b in range(3):
                pick(nc, ncs, 128 * b, 128, wb, wbs, 512, "ofs", 8 * b)
                scores(1, b)
        else:
            tags()
            mm(2, 128, ("wq", "ws", 0), (wb, wbs, 448))
            pick_rows("yw", 448, 64, "yw", 448, "ofa", 0)
            act(("yw", 512, 576), bank(2, 0, 64), F.Copy)
            pick_rows(ncs, 0, 192, wbs, 512, "ofs", 0)
            pick_rows("ysb", 192, 192, "yw", 512, "ofs", 12, 64)
            pick_rows(ncs, 192, 192, wbs, 512, "ofs", 12)
            for b in range(2):
                pick_codes(nc, 192 * b, 192, wb, 512, "ofs", 12 * b)
                dma(None, T.oc[:, 768 * b:768 * b + 768], T[nc][:, 192 * b:192 * b + 192].bitcast(dt.uint8),
                    [(nc, 192 * b, 192 * b + 192)], [])
            dma(None, T.y[:, 192:384], T.ysb[:, 192:384], [("ysb", 192, 384)], [])
            pick_rows("ysb", 0, 192, "yw", 512, "ofs", 0, 64)
            for k in range(4):
                dma(None, T.osc[4 * k:4 * k + 4, :], T[ncs][32 * k:32 * k + 4, 0:384], [whole(ncs)], [])
            dma(None, T.y[:, 0:192], T.ysb[:, 0:192], [("ysb", 0, 192)], [])
    for i in (ORDER.split() if ORDER else range(len(calls))):
        calls[int(i)][1]()
    for s in SEMAPHORES:
        if count[s]:
            g.wait_ge(T.sem[s], count[s])
